import numpy as np
import ml_dtypes


def mxq(x, axis, fmt="e4m3"):
    dtype, down = {"e4m3": (ml_dtypes.float8_e4m3fn, 7), "e5m2": (ml_dtypes.float8_e5m2, 14)}[fmt]
    v = np.moveaxis(np.asarray(x, np.float32).astype(ml_dtypes.bfloat16).astype(np.float64), axis, -1)
    blocks = v.reshape(v.shape[:-1] + (-1, 32))
    amax = np.abs(blocks).max(-1, keepdims=True)
    byte = np.maximum(np.where(amax > 0, np.frexp(amax)[1] - 1 + 127, 0) - down, 1)
    scale = np.exp2(byte - 127.0)
    codes = (blocks / scale).astype(np.float32).astype(dtype).astype(np.float64)
    return np.moveaxis((codes * scale).reshape(v.shape), -1, axis)


WIDE = False


def mx_kscale(k):
    if not WIDE:
        return np.ones(k)
    levels = np.array([10, -10, 5, -5, 0])
    if k % 512:
        return np.exp2(np.random.permutation(np.resize(levels, k // 32))).repeat(32)
    a = np.empty((k // 512, 16))
    for p in range(k // 512):
        a[p, :8] = np.random.permutation(np.resize(levels, 8))
        for g in range(8):
            far = levels[np.abs(levels - a[p, g]) >= 10]
            a[p, g + 8] = far[np.random.randint(len(far))]
    return np.exp2(a.ravel()).repeat(32)


def f64(x):
    return np.asarray(x).astype(np.float64)


def striped(idx):
    return np.tile(idx.reshape(-1, 16).T, (8, 1)).astype(np.uint16)


def unstriped(offs):
    return offs[:16].T.reshape(-1).astype(np.int64)


E2M1 = np.array([0.0, 0.5, 1.0, 1.5, 2.0, 3.0, 4.0, 6.0, -0.0, -0.5, -1.0, -1.5, -2.0, -3.0, -4.0, -6.0])


def pack_weight(w, fmt):
    k, n = w.shape
    w = f64(np.asarray(w, np.float32).astype(ml_dtypes.bfloat16)).reshape(k // 32, 32, n)
    amax = np.abs(w).max(1)
    if fmt == "e4m3":
        byte = np.frexp(amax)[1] - 1 + 127 - 7
    else:
        mant, ex = np.frexp(amax / 6.0)
        byte = np.where(mant > 0.5, ex, ex - 1) + 127
    byte = np.clip(np.where(amax > 0, byte, 1), 1, 254)
    scaled = (w * np.exp2(127.0 - byte)[:, None, :]).reshape(k, n).astype(np.float32)
    by_word = np.ascontiguousarray(scaled.reshape(k // 512, 128, 4, n).transpose(0, 1, 3, 2))
    if fmt == "e4m3":
        words = by_word.astype(ml_dtypes.float8_e4m3fn).view(np.uint8)
    else:
        c = by_word.astype(ml_dtypes.float4_e2m1fn).view(np.uint8) & 0xF
        words = (c[..., 0::2] | (c[..., 1::2] << 4)).reshape(k // 512, 128, 2 * n)
    return np.ascontiguousarray(words), np.ascontiguousarray(byte.astype(np.uint8).reshape(k // 512, 16, n))


def unpack_weight(words, scales, fmt):
    g, _, n = scales.shape
    words = np.ascontiguousarray(words).reshape(g, 128, n, -1)
    if fmt == "e4m3":
        vals = words.view(ml_dtypes.float8_e4m3fn).astype(np.float64)
    else:
        nib = np.empty((g, 128, n, 4), np.uint8)
        nib[..., 0::2] = words & 0xF
        nib[..., 1::2] = words >> 4
        vals = E2M1[nib]
    vals = vals * np.repeat(np.exp2(scales.astype(np.float64) - 127.0), 8, axis=1)[..., None]
    return vals.transpose(0, 1, 3, 2).reshape(g * 512, n)


def gelu(v):
    return 0.5 * v * (1.0 + np.tanh(np.sqrt(2.0 / np.pi) * (v + 0.044715 * v**3)))


K, T, S, H, N = 1024, 2048, 1024, 512, 1024


def setup_inputs():
    n = np.random.standard_normal
    s = mx_kscale(K)[:, None]
    u = mx_kscale(H)[:, None]
    tab_words, tab_scales = pack_weight(n((K, T)) * s, "e4m3")
    w1 = n((K, H)) / np.sqrt(K) / s * u.T
    wa_words, wa_scales = pack_weight(n((H, N)) / np.sqrt(H) / u, "e2m1")
    wb_words, wb_scales = pack_weight(n((K, N)) / np.sqrt(K) / s, "e4m3")
    return {
        "tab_words": tab_words, "tab_scales": tab_scales,
        "offs": striped(np.random.permutation(T)[:S]),
        "w1": w1.astype(np.float32),
        "wa_words": wa_words, "wa_scales": wa_scales,
        "wb_words": wb_words, "wb_scales": wb_scales,
        "gT": n((N, T)).astype(np.float32),
    }


def reference(tab_words, tab_scales, offs, w1, wa_words, wa_scales, wb_words, wb_scales, gT):
    v = unpack_weight(tab_words, tab_scales, "e4m3")[:, unstriped(offs)]
    g = f64(gT)[:, unstriped(offs)]
    wa = unpack_weight(wa_words, wa_scales, "e2m1")
    wb = unpack_weight(wb_words, wb_scales, "e4m3")
    h = np.maximum(mxq(f64(w1), 0, "e4m3").T @ v, 0.0)
    A = wa.T @ mxq(h, 0, "e4m3")
    B = wb.T @ v
    return np.exp(-np.exp(A)) * g + B

@@ -1,0 +1,237 @@
+from contextlib import ExitStack
+
+import concourse.mybir as mybir
+
+K, T, S, H, N = 1024, 2048, 1024, 512, 1024
+FLOPS = 2 * S * (K * H + H * N + K * N)
+
+F32 = mybir.dt.float32
+BF16 = mybir.dt.bfloat16
+I32 = mybir.dt.int32
+U32 = mybir.dt.uint32
+U16 = mybir.dt.uint16
+U8 = mybir.dt.uint8
+FP8X4 = mybir.dt.float8_e4m3fn_x4
+FP4X4 = mybir.dt.float4_e2m1fn_x4
+ACT = mybir.ActivationFunctionType
+ALU = mybir.AluOpType
+
+P = 128
+PACK = 4
+PASSES = K // (P * PACK)
+TILES = N // P
+CHUNK = 128
+QUARTER = 256
+HALF = 512
+
+
+def tile_list_session_state_decay_kernel(
+    tc, tab_words, tab_scales, offs, w1, wa_words, wa_scales, wb_words, wb_scales, gT, out
+):
+    nc = tc.nc
+    with ExitStack() as ctx:
+        keep = ctx.enter_context(tc.tile_pool(name="keep", bufs=1))
+        ring = ctx.enter_context(tc.tile_pool(name="ring", bufs=3))
+        psum = ctx.enter_context(tc.psum_pool(name="psum", bufs=1))
+
+        offsets = keep.tile([P, S // 16], U16, name="offsets")
+        tab_w = [keep.tile([P, T], I32, name=f"tab_w{a}", align_bytes=64) for a in range(PASSES)]
+        tab_s = keep.tile([P, T // 4], I32, name="tab_s", align_bytes=64)
+        wa_s = keep.tile([P, N // 4], I32, name="wa_s", align_bytes=64)
+        wb_s = keep.tile([P, PASSES, N // 4], I32, name="wb_s", align_bytes=64)
+        w1_raw = [keep.tile([P, PACK, H], F32, name=f"w1_raw{a}") for a in range(PASSES)]
+        w1_bf = [keep.tile([P, PACK * H], BF16, name=f"w1_bf{a}", align_bytes=64) for a in range(PASSES)]
+        w1_q = [keep.tile([P, H], U32, name=f"w1_q{a}", align_bytes=64) for a in range(PASSES)]
+        w1_s = [keep.tile([P, H], U8, name=f"w1_s{a}", align_bytes=64) for a in range(PASSES)]
+        wa_w = keep.tile([P, 2 * N], U8, name="wa_w", align_bytes=64)
+        wb_w = [keep.tile([P, PASSES, N // 2], I32, name=f"wb_w{u}", align_bytes=64) for u in range(2)]
+        state = [keep.tile([P, T], F32, name=f"state{i}") for i in range(TILES)]
+        v_w = [keep.tile([P, S], U32, name=f"v_w{a}", align_bytes=64) for a in range(PASSES)]
+        v_s = keep.tile([P, S], U8, name="v_s", align_bytes=64)
+        h_q = keep.tile([P, S], U32, name="h_q", align_bytes=64)
+        h_s = keep.tile([P, S], U8, name="h_s", align_bytes=64)
+        h_bf = [keep.tile([P, 2, CHUNK * PACK], BF16, name=f"h_bf{q}", align_bytes=64) for q in range(4)]
+        new = [keep.tile([P, S], F32, name=f"new{i}") for i in range(TILES)]
+
+        for plane in (tab_s, wa_s, wb_s):
+            nc.vector.memset(plane[:], 0)
+
+        wb_view = wb_words.rearrange("a p n i -> p a (n i)")
+
+        def load_w1(a):
+            rows = w1[a * P * PACK : (a + 1) * P * PACK, :]
+            nc.sync.dma_start(w1_raw[a][:], rows.rearrange("(p j) c -> p j c", j=PACK))
+
+        def load_table(a):
+            nc.sync.dma_start(tab_w[a][:], tab_words[a].rearrange("p t i -> p (t i)").bitcast(I32))
+
+        def load_table_scales(r):
+            for a in range(PASSES):
+                nc.sync.dma_start(tab_s[4 * a + r : P : 32, :], tab_scales[a, r:16:4, :].bitcast(I32))
+
+        def load_state(i):
+            nc.sync.dma_start(state[i][:], gT[i * P : (i + 1) * P, :])
+
+        def load_wb(u):
+            nc.sync.dma_start(wb_w[u][:], wb_view[:, :, u * 2 * N : (u + 1) * 2 * N].bitcast(I32))
+
+        nc.sync.dma_start(offsets[:], offs)
+        load_w1(0)
+        load_table_scales(0)
+        load_table_scales(1)
+        load_w1(1)
+        load_table_scales(2)
+        load_table_scales(3)
+        load_table(0)
+        load_table(1)
+        for r in range(4):
+            nc.sync.dma_start(wa_s[r:P:32, :], wa_scales[0, r:16:4, :].bitcast(I32))
+        nc.sync.dma_start(wa_w[:].bitcast(I32), wa_words[0].bitcast(I32))
+        load_state(0)
+        load_state(1)
+        for r in range(4):
+            nc.sync.dma_start(wb_s[r:P:32, :, :], wb_scales[:, r:16:4, :].rearrange("a q n -> q a n").bitcast(I32))
+        load_wb(0)
+        load_state(2)
+        load_state(3)
+        load_wb(1)
+        for i in range(4, TILES):
+            load_state(i)
+
+        def cast_views(a):
+            dst = w1_bf[a][:].rearrange("p (t m j) -> p m t j", t=PACK, j=PACK)
+            src = w1_raw[a][:].rearrange("p j (m t) -> p m t j", t=PACK)
+            return dst, src
+
+        def quantize_w1(a):
+            nc.vector.quantize_mx(out=w1_q[a][:].bitcast(FP8X4), scales=w1_s[a][:], in_=w1_bf[a][:])
+
+        def listed(j0, width):
+            return offsets[:, j0 // 16 : (j0 + width) // 16]
+
+        def gather_words(a, j0, width):
+            nc.vector.tensor_copy(v_w[a][:, j0 : j0 + width], tab_w[a][:].bitcast(U32).indirect(listed(j0, width)))
+
+        def gather_scales(j0, width):
+            nc.vector.tensor_copy(v_s[:, j0 : j0 + width], tab_s[:].bitcast(U8).indirect(listed(j0, width)))
+
+        def hidden_chunk(c, on_vector):
+            cols = slice(c * CHUNK, (c + 1) * CHUNK)
+            acc = psum.tile([P, PACK, CHUNK], F32, name="h_acc", bufs=3)
+            for t in range(PACK):
+                r = slice(t * P, (t + 1) * P)
+                for a in range(PASSES):
+                    nc.tensor.matmul_mx(
+                        out=acc[:, t, :],
+                        lhsT=w1_q[a][:, r].bitcast(FP8X4),
+                        lhsT_scale=w1_s[a][:, r],
+                        rhs=v_w[a][:, cols].bitcast(FP8X4),
+                        rhs_scale=v_s[4 * a :, cols],
+                        start=(a == 0),
+                        stop=(a == PASSES - 1),
+                    )
+            dst = h_bf[c // 2][:, c % 2, :].rearrange("p (j t) -> p j t", t=PACK)
+            src = acc[:].rearrange("p t j -> p j t")
+            if on_vector:
+                nc.vector.tensor_scalar_max(dst, src, 0.0)
+            else:
+                nc.scalar.activation(dst, src, ACT.Relu)
+
+        def quantize_h(q):
+            cols = slice(q * QUARTER, (q + 1) * QUARTER)
+            nc.vector.quantize_mx(
+                out=h_q[:, cols].bitcast(FP8X4), scales=h_s[:, cols], in_=h_bf[q][:].rearrange("p c w -> p (c w)")
+            )
+
+        def decay_times_state(i, j0, width):
+            cols = slice(j0, j0 + width)
+            a_acc = psum.tile([P, HALF], F32, name="a_acc", bufs=2)
+            nc.tensor.matmul_mx(
+                out=a_acc[:, :width],
+                lhsT=wa_w[:, 2 * i * P : 2 * (i + 1) * P].bitcast(FP4X4),
+                lhsT_scale=wa_s[:].bitcast(U8)[:, i * P : (i + 1) * P],
+                rhs=h_q[:, cols].bitcast(FP8X4),
+                rhs_scale=h_s[:, cols],
+                start=True,
+                stop=True,
+            )
+            rate = ring.tile([P, HALF], F32, name="rate", bufs=2)
+            decay = ring.tile([P, HALF], F32, name="decay", bufs=4)
+            nc.scalar.activation(rate[:, :width], a_acc[:, :width], ACT.Exp)
+            nc.scalar.activation(decay[:, :width], rate[:, :width], ACT.Exp, scale=-1.0)
+            nc.vector.tensor_tensor(new[i][:, cols], state[i][:].indirect(listed(j0, width)), decay[:, :width], ALU.mult)
+
+        def add_token(i, j0, width):
+            cols = slice(j0, j0 + width)
+            b_acc = psum.tile([P, HALF], F32, name="b_acc", bufs=3)
+            u, n0 = divmod(i * P, N // 2)
+            for a in range(PASSES):
+                nc.tensor.matmul_mx(
+                    out=b_acc[:, :width],
+                    lhsT=wb_w[u][:, a, n0 : n0 + P].bitcast(FP8X4),
+                    lhsT_scale=wb_s[:, a, :].bitcast(U8)[:, i * P : (i + 1) * P],
+                    rhs=v_w[a][:, cols].bitcast(FP8X4),
+                    rhs_scale=v_s[4 * a :, cols],
+                    start=(a == 0),
+                    stop=(a == PASSES - 1),
+                )
+            nc.vector.tensor_tensor(new[i][:, cols], b_acc[:, :width], new[i][:, cols], ALU.add)
+
+        def store(i, j0, width):
+            nc.sync.dma_start(out[i * P : (i + 1) * P, j0 : j0 + width], new[i][:, j0 : j0 + width])
+
+        dst, src = cast_views(0)
+        nc.vector.tensor_copy(dst, src)
+        dst, src = cast_views(1)
+        nc.scalar.activation(dst, src, ACT.Copy)
+        gather_scales(0, HALF)
+        quantize_w1(0)
+        gather_words(0, 0, HALF)
+        quantize_w1(1)
+        gather_words(1, 0, QUARTER)
+        hidden_chunk(0, False)
+        hidden_chunk(1, False)
+        gather_words(1, QUARTER, QUARTER)
+        hidden_chunk(2, False)
+        quantize_h(0)
+        hidden_chunk(3, False)
+        gather_scales(HALF, HALF)
+        gather_words(0, HALF, HALF)
+        gather_words(1, HALF, QUARTER)
+        decay_times_state(0, 0, QUARTER)
+        quantize_h(1)
+        hidden_chunk(4, False)
+        hidden_chunk(5, False)
+        gather_words(1, 3 * QUARTER, QUARTER)
+        decay_times_state(0, QUARTER, QUARTER)
+        quantize_h(2)
+        hidden_chunk(6, False)
+        hidden_chunk(7, False)
+        decay_times_state(1, 0, HALF)
+        quantize_h(3)
+
+        units = [(0, HALF, HALF), (1, HALF, HALF)]
+        units += [(i, j0, HALF) for i in range(2, TILES - 1) for j0 in (0, HALF)]
+        units += [(TILES - 1, 0, HALF), (TILES - 1, HALF, QUARTER), (TILES - 1, 3 * QUARTER, QUARTER)]
+        pending = [(0, 0, HALF), (1, 0, HALF)]
+        added = {}
+
+        def finish(unit):
+            i, j0, width = unit
+            add_token(i, j0, width)
+            if i == TILES - 1:
+                store(i, j0, width)
+                return
+            added[i] = added.get(i, 0) + width
+            if added[i] == S:
+                store(i, 0, S)
+
+        for unit in units:
+            decay_times_state(*unit)
+            finish(pending[0])
+            pending = pending[1:] + [unit]
+            if len(pending) > 1:
+                finish(pending[0])
+                pending = pending[1:]
+        for unit in pending:
+            finish(unit)

@@ -54,7 +54,7 @@ def tile_list_session_state_decay_kernel(
         new = [keep.tile([P, S], F32, name=f"new{i}") for i in range(TILES)]
 
         for plane in (tab_s, wa_s, wb_s):
-            nc.vector.memset(plane[:], 0)
+            nc.gpsimd.memset(plane[:], 0)
 
         wb_view = wb_words.rearrange("a p n i -> p a (n i)")
 
@@ -76,13 +76,13 @@ def tile_list_session_state_decay_kernel(
             nc.sync.dma_start(wb_w[u][:], wb_view[:, :, u * 2 * N : (u + 1) * 2 * N].bitcast(I32))
 
         nc.sync.dma_start(offsets[:], offs)
-        load_w1(0)
+        load_table(0)
         load_table_scales(0)
         load_table_scales(1)
-        load_w1(1)
+        load_w1(0)
         load_table_scales(2)
         load_table_scales(3)
-        load_table(0)
+        load_w1(1)
         load_table(1)
         for r in range(4):
             nc.sync.dma_start(wa_s[r:P:32, :], wa_scales[0, r:16:4, :].bitcast(I32))
@@ -117,7 +117,7 @@ def tile_list_session_state_decay_kernel(
 
         def hidden_chunk(c, on_vector):
             cols = slice(c * CHUNK, (c + 1) * CHUNK)
-            acc = psum.tile([P, PACK, CHUNK], F32, name="h_acc", bufs=3)
+            acc = psum.tile([P, PACK, CHUNK], F32, name="h_acc", tag="acc", bufs=6)
             for t in range(PACK):
                 r = slice(t * P, (t + 1) * P)
                 for a in range(PASSES):
@@ -143,27 +143,33 @@ def tile_list_session_state_decay_kernel(
                 out=h_q[:, cols].bitcast(FP8X4), scales=h_s[:, cols], in_=h_bf[q][:].rearrange("p c w -> p (c w)")
             )
 
-        def decay_times_state(i, j0, width):
-            cols = slice(j0, j0 + width)
-            a_acc = psum.tile([P, HALF], F32, name="a_acc", bufs=2)
-            nc.tensor.matmul_mx(
-                out=a_acc[:, :width],
-                lhsT=wa_w[:, 2 * i * P : 2 * (i + 1) * P].bitcast(FP4X4),
-                lhsT_scale=wa_s[:].bitcast(U8)[:, i * P : (i + 1) * P],
-                rhs=h_q[:, cols].bitcast(FP8X4),
-                rhs_scale=h_s[:, cols],
-                start=True,
-                stop=True,
-            )
-            rate = ring.tile([P, HALF], F32, name="rate", bufs=2)
-            decay = ring.tile([P, HALF], F32, name="decay", bufs=4)
-            nc.scalar.activation(rate[:, :width], a_acc[:, :width], ACT.Exp)
+        def gather_state(i):
+            nc.vector.tensor_copy(new[i][:], state[i][:].indirect(offsets[:]))
+
+        def apply_decay(i, j0, width):
+            rate = ring.tile([P, S], F32, name="rate", bufs=2)
+            decay = ring.tile([P, S], F32, name="decay", bufs=4)
+            for c0 in range(0, width, HALF):
+                n = min(HALF, width - c0)
+                cols = slice(j0 + c0, j0 + c0 + n)
+                a_acc = psum.tile([P, HALF], F32, name="a_acc", bufs=2)
+                nc.tensor.matmul_mx(
+                    out=a_acc[:, :n],
+                    lhsT=wa_w[:, 2 * i * P : 2 * (i + 1) * P].bitcast(FP4X4),
+                    lhsT_scale=wa_s[:].bitcast(U8)[:, i * P : (i + 1) * P],
+                    rhs=h_q[:, cols].bitcast(FP8X4),
+                    rhs_scale=h_s[:, cols],
+                    start=True,
+                    stop=True,
+                )
+                nc.scalar.activation(rate[:, c0 : c0 + n], a_acc[:, :n], ACT.Exp)
             nc.scalar.activation(decay[:, :width], rate[:, :width], ACT.Exp, scale=-1.0)
-            nc.vector.tensor_tensor(new[i][:, cols], state[i][:].indirect(listed(j0, width)), decay[:, :width], ALU.mult)
+            cols = slice(j0, j0 + width)
+            nc.gpsimd.tensor_tensor(new[i][:, cols], new[i][:, cols], decay[:, :width], ALU.mult)
 
         def add_token(i, j0, width):
             cols = slice(j0, j0 + width)
-            b_acc = psum.tile([P, HALF], F32, name="b_acc", bufs=3)
+            b_acc = psum.tile([P, HALF], F32, name="b_acc", tag="acc", bufs=6)
             u, n0 = divmod(i * P, N // 2)
             for a in range(PASSES):
                 nc.tensor.matmul_mx(
@@ -175,63 +181,42 @@ def tile_list_session_state_decay_kernel(
                     start=(a == 0),
                     stop=(a == PASSES - 1),
                 )
-            nc.vector.tensor_tensor(new[i][:, cols], b_acc[:, :width], new[i][:, cols], ALU.add)
+            nc.vector.tensor_tensor(new[i][:, cols], new[i][:, cols], b_acc[:, :width], ALU.add)
 
         def store(i, j0, width):
             nc.sync.dma_start(out[i * P : (i + 1) * P, j0 : j0 + width], new[i][:, j0 : j0 + width])
 
+        gather_words(0, 0, S)
         dst, src = cast_views(0)
-        nc.vector.tensor_copy(dst, src)
-        dst, src = cast_views(1)
         nc.scalar.activation(dst, src, ACT.Copy)
-        gather_scales(0, HALF)
+        gather_scales(0, S)
+        dst, src = cast_views(1)
+        nc.vector.tensor_copy(dst, src)
         quantize_w1(0)
-        gather_words(0, 0, HALF)
         quantize_w1(1)
-        gather_words(1, 0, QUARTER)
-        hidden_chunk(0, False)
-        hidden_chunk(1, False)
-        gather_words(1, QUARTER, QUARTER)
-        hidden_chunk(2, False)
-        quantize_h(0)
-        hidden_chunk(3, False)
-        gather_scales(HALF, HALF)
-        gather_words(0, HALF, HALF)
-        gather_words(1, HALF, QUARTER)
-        decay_times_state(0, 0, QUARTER)
-        quantize_h(1)
-        hidden_chunk(4, False)
-        hidden_chunk(5, False)
-        gather_words(1, 3 * QUARTER, QUARTER)
-        decay_times_state(0, QUARTER, QUARTER)
-        quantize_h(2)
-        hidden_chunk(6, False)
-        hidden_chunk(7, False)
-        decay_times_state(1, 0, HALF)
-        quantize_h(3)
+        for q in range(4):
+            gather_words(1, q * QUARTER, QUARTER)
+        for q in range(4):
+            hidden_chunk(2 * q, False)
+            hidden_chunk(2 * q + 1, False)
+            quantize_h(q)
 
-        units = [(0, HALF, HALF), (1, HALF, HALF)]
-        units += [(i, j0, HALF) for i in range(2, TILES - 1) for j0 in (0, HALF)]
-        units += [(TILES - 1, 0, HALF), (TILES - 1, HALF, QUARTER), (TILES - 1, 3 * QUARTER, QUARTER)]
-        pending = [(0, 0, HALF), (1, 0, HALF)]
-        added = {}
-
-        def finish(unit):
-            i, j0, width = unit
-            add_token(i, j0, width)
-            if i == TILES - 1:
-                store(i, j0, width)
-                return
-            added[i] = added.get(i, 0) + width
-            if added[i] == S:
-                store(i, 0, S)
-
-        for unit in units:
-            decay_times_state(*unit)
-            finish(pending[0])
-            pending = pending[1:] + [unit]
-            if len(pending) > 1:
-                finish(pending[0])
-                pending = pending[1:]
-        for unit in pending:
-            finish(unit)
+        lead = 5
+        for i in range(lead):
+            gather_state(i)
+        apply_decay(0, 0, HALF)
+        apply_decay(0, HALF, HALF)
+        for i in range(1, TILES):
+            if i < TILES - 1:
+                apply_decay(i, 0, S)
+            else:
+                apply_decay(i, 0, HALF)
+                apply_decay(i, HALF, HALF)
+            add_token(i - 1, 0, HALF)
+            add_token(i - 1, HALF, HALF)
+            store(i - 1, 0, S)
+            if i - 1 + lead < TILES:
+                gather_state(i - 1 + lead)
+        for j0, width in ((0, HALF), (HALF, QUARTER), (3 * QUARTER, QUARTER)):
+            add_token(TILES - 1, j0, width)
+            store(TILES - 1, j0, width)

@@ -23,6 +23,7 @@ TILES = N // P
 CHUNK = 128
 QUARTER = 256
 HALF = 512
+WB_PIECES = ((0, 1), (1, 3), (3, 5), (5, 8))
 
 
 def tile_list_session_state_decay_kernel(
@@ -44,7 +45,7 @@ def tile_list_session_state_decay_kernel(
         w1_q = [keep.tile([P, H], U32, name=f"w1_q{a}", align_bytes=64) for a in range(PASSES)]
         w1_s = [keep.tile([P, H], U8, name=f"w1_s{a}", align_bytes=64) for a in range(PASSES)]
         wa_w = keep.tile([P, 2 * N], U8, name="wa_w", align_bytes=64)
-        wb_w = [keep.tile([P, PASSES, N // 2], I32, name=f"wb_w{u}", align_bytes=64) for u in range(2)]
+        wb_w = [keep.tile([P, PASSES, (b - a) * P], I32, name=f"wb_w{a}", align_bytes=64) for a, b in WB_PIECES]
         state = [keep.tile([P, T], F32, name=f"state{i}") for i in range(TILES)]
         v_w = [keep.tile([P, S], U32, name=f"v_w{a}", align_bytes=64) for a in range(PASSES)]
         v_s = keep.tile([P, S], U8, name="v_s", align_bytes=64)
@@ -54,7 +55,7 @@ def tile_list_session_state_decay_kernel(
         new = [keep.tile([P, S], F32, name=f"new{i}") for i in range(TILES)]
 
         for plane in (tab_s, wa_s, wb_s):
-            nc.gpsimd.memset(plane[:], 0)
+            nc.vector.memset(plane[:], 0)
 
         wb_view = wb_words.rearrange("a p n i -> p a (n i)")
 
@@ -65,23 +66,21 @@ def tile_list_session_state_decay_kernel(
         def load_table(a):
             nc.sync.dma_start(tab_w[a][:], tab_words[a].rearrange("p t i -> p (t i)").bitcast(I32))
 
-        def load_table_scales(r):
-            for a in range(PASSES):
-                nc.sync.dma_start(tab_s[4 * a + r : P : 32, :], tab_scales[a, r:16:4, :].bitcast(I32))
+        def load_table_scales(q):
+            nc.sync.dma_start(tab_s[32 * q : 32 * q + 8, :], tab_scales[:, 4 * q : 4 * q + 4, :].bitcast(I32))
 
         def load_state(i):
             nc.sync.dma_start(state[i][:], gT[i * P : (i + 1) * P, :])
 
         def load_wb(u):
-            nc.sync.dma_start(wb_w[u][:], wb_view[:, :, u * 2 * N : (u + 1) * 2 * N].bitcast(I32))
+            first, end = WB_PIECES[u]
+            nc.sync.dma_start(wb_w[u][:], wb_view[:, :, first * P * PACK : end * P * PACK].bitcast(I32))
 
         nc.sync.dma_start(offsets[:], offs)
-        load_table(0)
-        load_table_scales(0)
-        load_table_scales(1)
         load_w1(0)
-        load_table_scales(2)
-        load_table_scales(3)
+        for q in range(4):
+            load_table_scales(q)
+        load_table(0)
         load_w1(1)
         load_table(1)
         for r in range(4):
@@ -93,10 +92,12 @@ def tile_list_session_state_decay_kernel(
             nc.sync.dma_start(wb_s[r:P:32, :, :], wb_scales[:, r:16:4, :].rearrange("a q n -> q a n").bitcast(I32))
         load_wb(0)
         load_state(2)
-        load_state(3)
         load_wb(1)
-        for i in range(4, TILES):
-            load_state(i)
+        for u in (2, 3):
+            load_state(2 * u - 1)
+            load_state(2 * u)
+            load_wb(u)
+        load_state(TILES - 1)
 
         def cast_views(a):
             dst = w1_bf[a][:].rearrange("p (t m j) -> p m t j", t=PACK, j=PACK)
@@ -115,23 +116,25 @@ def tile_list_session_state_decay_kernel(
         def gather_scales(j0, width):
             nc.vector.tensor_copy(v_s[:, j0 : j0 + width], tab_s[:].bitcast(U8).indirect(listed(j0, width)))
 
-        def hidden_chunk(c, on_vector):
+        h_acc = [psum.tile([P, PACK, CHUNK], F32, name=f"h_acc{c}", tag="bank", bufs=8) for c in range(S // CHUNK)]
+
+        def hidden_pass(c, a):
             cols = slice(c * CHUNK, (c + 1) * CHUNK)
-            acc = psum.tile([P, PACK, CHUNK], F32, name="h_acc", tag="acc", bufs=6)
             for t in range(PACK):
                 r = slice(t * P, (t + 1) * P)
-                for a in range(PASSES):
-                    nc.tensor.matmul_mx(
-                        out=acc[:, t, :],
-                        lhsT=w1_q[a][:, r].bitcast(FP8X4),
-                        lhsT_scale=w1_s[a][:, r],
-                        rhs=v_w[a][:, cols].bitcast(FP8X4),
-                        rhs_scale=v_s[4 * a :, cols],
-                        start=(a == 0),
-                        stop=(a == PASSES - 1),
-                    )
+                nc.tensor.matmul_mx(
+                    out=h_acc[c][:, t, :],
+                    lhsT=w1_q[a][:, r].bitcast(FP8X4),
+                    lhsT_scale=w1_s[a][:, r],
+                    rhs=v_w[a][:, cols].bitcast(FP8X4),
+                    rhs_scale=v_s[4 * a :, cols],
+                    start=(a == 0 and t == 0),
+                    stop=(a == PASSES - 1 and t == PACK - 1),
+                )
+
+        def relu(c, on_vector):
             dst = h_bf[c // 2][:, c % 2, :].rearrange("p (j t) -> p j t", t=PACK)
-            src = acc[:].rearrange("p t j -> p j t")
+            src = h_acc[c][:].rearrange("p t j -> p j t")
             if on_vector:
                 nc.vector.tensor_scalar_max(dst, src, 0.0)
             else:
@@ -143,16 +146,13 @@ def tile_list_session_state_decay_kernel(
                 out=h_q[:, cols].bitcast(FP8X4), scales=h_s[:, cols], in_=h_bf[q][:].rearrange("p c w -> p (c w)")
             )
 
-        def gather_state(i):
-            nc.vector.tensor_copy(new[i][:], state[i][:].indirect(offsets[:]))
-
         def apply_decay(i, j0, width):
             rate = ring.tile([P, S], F32, name="rate", bufs=2)
             decay = ring.tile([P, S], F32, name="decay", bufs=4)
             for c0 in range(0, width, HALF):
                 n = min(HALF, width - c0)
                 cols = slice(j0 + c0, j0 + c0 + n)
-                a_acc = psum.tile([P, HALF], F32, name="a_acc", bufs=2)
+                a_acc = psum.tile([P, HALF], F32, name="a_acc", tag="bank", bufs=8)
                 nc.tensor.matmul_mx(
                     out=a_acc[:, :n],
                     lhsT=wa_w[:, 2 * i * P : 2 * (i + 1) * P].bitcast(FP4X4),
@@ -165,12 +165,13 @@ def tile_list_session_state_decay_kernel(
                 nc.scalar.activation(rate[:, c0 : c0 + n], a_acc[:, :n], ACT.Exp)
             nc.scalar.activation(decay[:, :width], rate[:, :width], ACT.Exp, scale=-1.0)
             cols = slice(j0, j0 + width)
-            nc.gpsimd.tensor_tensor(new[i][:, cols], new[i][:, cols], decay[:, :width], ALU.mult)
+            nc.vector.tensor_tensor(new[i][:, cols], state[i][:].indirect(listed(j0, width)), decay[:, :width], ALU.mult)
 
         def add_token(i, j0, width):
             cols = slice(j0, j0 + width)
-            b_acc = psum.tile([P, HALF], F32, name="b_acc", tag="acc", bufs=6)
-            u, n0 = divmod(i * P, N // 2)
+            b_acc = psum.tile([P, HALF], F32, name="b_acc", tag="bank", bufs=8)
+            u = min((i + 1) // 2, len(WB_PIECES) - 1)
+            n0 = (i - WB_PIECES[u][0]) * P
             for a in range(PASSES):
                 nc.tensor.matmul_mx(
                     out=b_acc[:, :width],
@@ -181,42 +182,52 @@ def tile_list_session_state_decay_kernel(
                     start=(a == 0),
                     stop=(a == PASSES - 1),
                 )
-            nc.vector.tensor_tensor(new[i][:, cols], new[i][:, cols], b_acc[:, :width], ALU.add)
+            nc.vector.tensor_tensor(new[i][:, cols], b_acc[:, :width], new[i][:, cols], ALU.add)
 
         def store(i, j0, width):
             nc.sync.dma_start(out[i * P : (i + 1) * P, j0 : j0 + width], new[i][:, j0 : j0 + width])
 
-        gather_words(0, 0, S)
         dst, src = cast_views(0)
         nc.scalar.activation(dst, src, ACT.Copy)
         gather_scales(0, S)
-        dst, src = cast_views(1)
-        nc.vector.tensor_copy(dst, src)
         quantize_w1(0)
+        gather_words(0, 0, HALF)
+        gather_words(0, HALF, HALF)
+        dst, src = cast_views(1)
+        nc.scalar.activation(dst[:, : P // 2], src[:, : P // 2], ACT.Copy)
+        nc.vector.tensor_copy(dst[:, P // 2 :], src[:, P // 2 :])
         quantize_w1(1)
+        for c in range(S // CHUNK):
+            hidden_pass(c, 0)
         for q in range(4):
             gather_words(1, q * QUARTER, QUARTER)
         for q in range(4):
-            hidden_chunk(2 * q, False)
-            hidden_chunk(2 * q + 1, False)
+            for c in (2 * q, 2 * q + 1):
+                hidden_pass(c, 1)
+                relu(c, c in (3, 5, 7))
             quantize_h(q)
+            if q == 1:
+                apply_decay(0, 0, HALF)
+            elif q > 1:
+                apply_decay(0, q * QUARTER, QUARTER)
 
-        lead = 5
-        for i in range(lead):
-            gather_state(i)
-        apply_decay(0, 0, HALF)
-        apply_decay(0, HALF, HALF)
-        for i in range(1, TILES):
-            if i < TILES - 1:
-                apply_decay(i, 0, S)
-            else:
-                apply_decay(i, 0, HALF)
-                apply_decay(i, HALF, HALF)
-            add_token(i - 1, 0, HALF)
-            add_token(i - 1, HALF, HALF)
-            store(i - 1, 0, S)
-            if i - 1 + lead < TILES:
-                gather_state(i - 1 + lead)
+        apply_decay(1, 0, HALF)
+        apply_decay(1, HALF, HALF)
+
+        def finish(i):
+            add_token(i, 0, HALF)
+            add_token(i, HALF, HALF)
+            store(i, 0, S)
+
+        finish(0)
+        for i in range(2, TILES - 1):
+            apply_decay(i, 0, S)
+            if i % 2 == 0:
+                finish(i - 1)
+                finish(i)
+        last = TILES - 1
+        apply_decay(last, 0, HALF)
+        apply_decay(last, HALF, HALF)
         for j0, width in ((0, HALF), (HALF, QUARTER), (3 * QUARTER, QUARTER)):
-            add_token(TILES - 1, j0, width)
-            store(TILES - 1, j0, width)
+            add_token(last, j0, width)
+            store(last, j0, width)

@@ -37,12 +37,11 @@ def tile_list_session_state_decay_kernel(
 
         offsets = keep.tile([P, S // 16], U16, name="offsets")
         tab_w = [keep.tile([P, T], I32, name=f"tab_w{a}", align_bytes=64) for a in range(PASSES)]
-        tab_s = keep.tile([P, T // 4], I32, name="tab_s", align_bytes=64)
+        tab_s = keep.tile([P, T // 4], I32, name="tab_s", tag="w1_q0", align_bytes=64)
         wa_s = keep.tile([P, N // 4], I32, name="wa_s", align_bytes=64)
         wb_s = keep.tile([P, PASSES, N // 4], I32, name="wb_s", align_bytes=64)
         w1_raw = [keep.tile([P, PACK, H], F32, name=f"w1_raw{a}") for a in range(PASSES)]
         w1_bf = [keep.tile([P, PACK * H], BF16, name=f"w1_bf{a}", align_bytes=64) for a in range(PASSES)]
-        w1_q = [keep.tile([P, H], U32, name=f"w1_q{a}", align_bytes=64) for a in range(PASSES)]
         w1_s = [keep.tile([P, H], U8, name=f"w1_s{a}", align_bytes=64) for a in range(PASSES)]
         wa_w = keep.tile([P, 2 * N], U8, name="wa_w", align_bytes=64)
         wb_w = [keep.tile([P, PASSES, (b - a) * P], I32, name=f"wb_w{a}", align_bytes=64) for a, b in WB_PIECES]
@@ -66,8 +65,9 @@ def tile_list_session_state_decay_kernel(
         def load_table(a):
             nc.sync.dma_start(tab_w[a][:], tab_words[a].rearrange("p t i -> p (t i)").bitcast(I32))
 
-        def load_table_scales(q):
-            nc.sync.dma_start(tab_s[32 * q : 32 * q + 8, :], tab_scales[:, 4 * q : 4 * q + 4, :].bitcast(I32))
+        def load_table_scales(q, first, end):
+            rows = tab_scales[first:end, 4 * q : 4 * q + 4, :]
+            nc.sync.dma_start(tab_s[32 * q + 4 * first : 32 * q + 4 * end, :], rows.bitcast(I32))
 
         def load_state(i):
             nc.sync.dma_start(state[i][:], gT[i * P : (i + 1) * P, :])
@@ -79,7 +79,7 @@ def tile_list_session_state_decay_kernel(
         nc.sync.dma_start(offsets[:], offs)
         load_w1(0)
         for q in range(4):
-            load_table_scales(q)
+            load_table_scales(q, 0, 2)
         load_table(0)
         load_w1(1)
         load_table(1)
@@ -99,12 +99,16 @@ def tile_list_session_state_decay_kernel(
             load_wb(u)
         load_state(TILES - 1)
 
-        def cast_views(a):
+        def cast_w1(a, split):
             dst = w1_bf[a][:].rearrange("p (t m j) -> p m t j", t=PACK, j=PACK)
             src = w1_raw[a][:].rearrange("p j (m t) -> p m t j", t=PACK)
-            return dst, src
+            nc.scalar.activation(dst[:, :split], src[:, :split], ACT.Copy)
+            nc.vector.tensor_copy(dst[:, split:], src[:, split:])
+
+        w1_q = {}
 
         def quantize_w1(a):
+            w1_q[a] = keep.tile([P, H], U32, name=f"w1_q{a}", tag=f"w1_q{a}", align_bytes=64)
             nc.vector.quantize_mx(out=w1_q[a][:].bitcast(FP8X4), scales=w1_s[a][:], in_=w1_bf[a][:])
 
         def listed(j0, width):
@@ -187,15 +191,12 @@ def tile_list_session_state_decay_kernel(
         def store(i, j0, width):
             nc.sync.dma_start(out[i * P : (i + 1) * P, j0 : j0 + width], new[i][:, j0 : j0 + width])
 
-        dst, src = cast_views(0)
-        nc.scalar.activation(dst, src, ACT.Copy)
+        cast_w1(0, 96)
         gather_scales(0, S)
         quantize_w1(0)
         gather_words(0, 0, HALF)
         gather_words(0, HALF, HALF)
-        dst, src = cast_views(1)
-        nc.scalar.activation(dst[:, : P // 2], src[:, : P // 2], ACT.Copy)
-        nc.vector.tensor_copy(dst[:, P // 2 :], src[:, P // 2 :])
+        cast_w1(1, 64)
         quantize_w1(1)
         for c in range(S // CHUNK):
             hidden_pass(c, 0)
@@ -227,7 +228,10 @@ def tile_list_session_state_decay_kernel(
                 finish(i)
         last = TILES - 1
         apply_decay(last, 0, HALF)
-        apply_decay(last, HALF, HALF)
-        for j0, width in ((0, HALF), (HALF, QUARTER), (3 * QUARTER, QUARTER)):
-            add_token(last, j0, width)
-            store(last, j0, width)
+        apply_decay(last, HALF, QUARTER)
+        add_token(last, 0, HALF)
+        store(last, 0, HALF)
+        apply_decay(last, 3 * QUARTER, QUARTER)
+        for j0 in (HALF, 3 * QUARTER):
+            add_token(last, j0, QUARTER)
+            store(last, j0, QUARTER)

@@ -23,7 +23,9 @@ TILES = N // P
 CHUNK = 128
 QUARTER = 256
 HALF = 512
-WB_PIECES = ((0, 1), (1, 3), (3, 5), (5, 8))
+ROW_GAP = 8
+GATHER_ROWS = ((0, 5), (5, 8))
+ADD_ON_GPSIMD = ((0, 1), (2, 1))
 
 
 def tile_list_session_state_decay_kernel(
@@ -32,7 +34,6 @@ def tile_list_session_state_decay_kernel(
     nc = tc.nc
     with ExitStack() as ctx:
         keep = ctx.enter_context(tc.tile_pool(name="keep", bufs=1))
-        ring = ctx.enter_context(tc.tile_pool(name="ring", bufs=3))
         psum = ctx.enter_context(tc.psum_pool(name="psum", bufs=1))
 
         offsets = keep.tile([P, S // 16], U16, name="offsets")
@@ -44,13 +45,15 @@ def tile_list_session_state_decay_kernel(
         w1_bf = [keep.tile([P, PACK * H], BF16, name=f"w1_bf{a}", align_bytes=64) for a in range(PASSES)]
         w1_s = [keep.tile([P, H], U8, name=f"w1_s{a}", align_bytes=64) for a in range(PASSES)]
         wa_w = keep.tile([P, 2 * N], U8, name="wa_w", align_bytes=64)
-        wb_w = [keep.tile([P, PASSES, (b - a) * P], I32, name=f"wb_w{a}", align_bytes=64) for a, b in WB_PIECES]
+        wb_w = [keep.tile([P, PASSES, 2 * P], I32, name=f"wb_w{u}", align_bytes=64) for u in range(TILES // 2)]
         state = [keep.tile([P, T], F32, name=f"state{i}") for i in range(TILES)]
         v_w = [keep.tile([P, S], U32, name=f"v_w{a}", align_bytes=64) for a in range(PASSES)]
         v_s = keep.tile([P, S], U8, name="v_s", align_bytes=64)
         h_q = keep.tile([P, S], U32, name="h_q", align_bytes=64)
         h_s = keep.tile([P, S], U8, name="h_s", align_bytes=64)
-        h_bf = [keep.tile([P, 2, CHUNK * PACK], BF16, name=f"h_bf{q}", align_bytes=64) for q in range(4)]
+        h_bf = [
+            keep.tile([P, 4, CHUNK * PACK], BF16, name=f"h_bf{u}", tag=f"stage{u + 2}", align_bytes=64) for u in range(2)
+        ]
         new = [keep.tile([P, S], F32, name=f"new{i}") for i in range(TILES)]
 
         for plane in (tab_s, wa_s, wb_s):
@@ -58,9 +61,9 @@ def tile_list_session_state_decay_kernel(
 
         wb_view = wb_words.rearrange("a p n i -> p a (n i)")
 
-        def load_w1(a):
+        def load_w1(a, first, end):
             rows = w1[a * P * PACK : (a + 1) * P * PACK, :]
-            nc.sync.dma_start(w1_raw[a][:], rows.rearrange("(p j) c -> p j c", j=PACK))
+            nc.sync.dma_start(w1_raw[a][:, first:end, :], rows.rearrange("(p j) c -> p j c", j=PACK)[:, first:end, :])
 
         def load_table(a):
             nc.sync.dma_start(tab_w[a][:], tab_words[a].rearrange("p t i -> p (t i)").bitcast(I32))
@@ -73,31 +76,31 @@ def tile_list_session_state_decay_kernel(
             nc.sync.dma_start(state[i][:], gT[i * P : (i + 1) * P, :])
 
         def load_wb(u):
-            first, end = WB_PIECES[u]
-            nc.sync.dma_start(wb_w[u][:], wb_view[:, :, first * P * PACK : end * P * PACK].bitcast(I32))
+            nc.sync.dma_start(wb_w[u][:], wb_view[:, :, 2 * u * P * PACK : 2 * (u + 1) * P * PACK].bitcast(I32))
 
         nc.sync.dma_start(offsets[:], offs)
-        load_w1(0)
+        load_w1(0, 0, 2)
         for q in range(4):
             load_table_scales(q, 0, 2)
+        load_w1(0, 2, 4)
         load_table(0)
-        load_w1(1)
-        load_table(1)
         for r in range(4):
             nc.sync.dma_start(wa_s[r:P:32, :], wa_scales[0, r:16:4, :].bitcast(I32))
-        nc.sync.dma_start(wa_w[:].bitcast(I32), wa_words[0].bitcast(I32))
+        load_w1(1, 0, 4)
+        load_table(1)
         load_state(0)
         load_state(1)
         for r in range(4):
             nc.sync.dma_start(wb_s[r:P:32, :, :], wb_scales[:, r:16:4, :].rearrange("a q n -> q a n").bitcast(I32))
-        load_wb(0)
+        nc.sync.dma_start(wa_w[:].bitcast(I32), wa_words[0].bitcast(I32))
         load_state(2)
-        load_wb(1)
-        for u in (2, 3):
-            load_state(2 * u - 1)
-            load_state(2 * u)
+        load_state(3)
+        load_wb(0)
+        for u in (1, 2):
+            load_state(2 * u + 2)
+            load_state(2 * u + 3)
             load_wb(u)
-        load_state(TILES - 1)
+        load_wb(3)
 
         def cast_w1(a, split):
             dst = w1_bf[a][:].rearrange("p (t m j) -> p m t j", t=PACK, j=PACK)
@@ -120,7 +123,7 @@ def tile_list_session_state_decay_kernel(
         def gather_scales(j0, width):
             nc.vector.tensor_copy(v_s[:, j0 : j0 + width], tab_s[:].bitcast(U8).indirect(listed(j0, width)))
 
-        h_acc = [psum.tile([P, PACK, CHUNK], F32, name=f"h_acc{c}", tag="bank", bufs=8) for c in range(S // CHUNK)]
+        h_acc = [psum.tile([P, PACK, CHUNK], F32, name=f"h_acc{c}", tag=f"bank{c}") for c in range(S // CHUNK)]
 
         def hidden_pass(c, a):
             cols = slice(c * CHUNK, (c + 1) * CHUNK)
@@ -136,27 +139,35 @@ def tile_list_session_state_decay_kernel(
                     stop=(a == PASSES - 1 and t == PACK - 1),
                 )
 
-        def relu(c, on_vector):
-            dst = h_bf[c // 2][:, c % 2, :].rearrange("p (j t) -> p j t", t=PACK)
+        def relu(c):
+            dst = h_bf[c // 4][:, c % 4, :].rearrange("p (j t) -> p j t", t=PACK)
             src = h_acc[c][:].rearrange("p t j -> p j t")
-            if on_vector:
-                nc.vector.tensor_scalar_max(dst, src, 0.0)
-            else:
-                nc.scalar.activation(dst, src, ACT.Relu)
+            nc.scalar.activation(dst, src, ACT.Relu)
 
         def quantize_h(q):
-            cols = slice(q * QUARTER, (q + 1) * QUARTER)
+            cols = slice(q * HALF, (q + 1) * HALF)
             nc.vector.quantize_mx(
                 out=h_q[:, cols].bitcast(FP8X4), scales=h_s[:, cols], in_=h_bf[q][:].rearrange("p c w -> p (c w)")
             )
 
-        def apply_decay(i, j0, width):
-            rate = ring.tile([P, S], F32, name="rate", bufs=2)
-            decay = ring.tile([P, S], F32, name="decay", bufs=4)
+        picked = {}
+
+        def gather_state(i):
+            picked[i] = keep.tile(
+                [P, S // CHUNK, CHUNK + ROW_GAP], U32, name=f"picked{i}", tag=f"stage{i % 4}", align_bytes=64
+            )
+            for first, end in GATHER_ROWS:
+                nc.vector.tensor_copy(
+                    picked[i][:, first:end, :CHUNK],
+                    state[i][:].bitcast(U32).indirect(listed(first * CHUNK, (end - first) * CHUNK)),
+                )
+
+        def apply_decay(i, j0, width, bank):
+            decay = new[i][:, j0 : j0 + width]
             for c0 in range(0, width, HALF):
                 n = min(HALF, width - c0)
                 cols = slice(j0 + c0, j0 + c0 + n)
-                a_acc = psum.tile([P, HALF], F32, name="a_acc", tag="bank", bufs=8)
+                a_acc = psum.tile([P, HALF], F32, name="a_acc", tag=f"bank{bank + c0 // HALF}")
                 nc.tensor.matmul_mx(
                     out=a_acc[:, :n],
                     lhsT=wa_w[:, 2 * i * P : 2 * (i + 1) * P].bitcast(FP4X4),
@@ -166,72 +177,83 @@ def tile_list_session_state_decay_kernel(
                     start=True,
                     stop=True,
                 )
-                nc.scalar.activation(rate[:, c0 : c0 + n], a_acc[:, :n], ACT.Exp)
-            nc.scalar.activation(decay[:, :width], rate[:, :width], ACT.Exp, scale=-1.0)
-            cols = slice(j0, j0 + width)
-            nc.vector.tensor_tensor(new[i][:, cols], state[i][:].indirect(listed(j0, width)), decay[:, :width], ALU.mult)
+                nc.scalar.activation(decay[:, c0 : c0 + n], a_acc[:, :n], ACT.Exp)
+            nc.scalar.activation(decay, decay, ACT.Exp, scale=-1.0)
+            rows = slice(j0 // CHUNK, (j0 + width) // CHUNK)
+            nc.gpsimd.tensor_tensor(
+                decay.rearrange("p (r c) -> p r c", c=CHUNK),
+                picked[i][:, rows, :CHUNK].bitcast(F32),
+                decay.rearrange("p (r c) -> p r c", c=CHUNK),
+                ALU.mult,
+            )
 
-        def add_token(i, j0, width):
-            cols = slice(j0, j0 + width)
-            b_acc = psum.tile([P, HALF], F32, name="b_acc", tag="bank", bufs=8)
-            u = min((i + 1) // 2, len(WB_PIECES) - 1)
-            n0 = (i - WB_PIECES[u][0]) * P
+        def token_product(i, half):
+            cols = slice(half * HALF, (half + 1) * HALF)
+            b_acc = psum.tile([P, HALF], F32, name="b_acc", tag=f"bank{2 + (2 * i + half) % 6}")
+            n0 = (i % 2) * P
             for a in range(PASSES):
                 nc.tensor.matmul_mx(
-                    out=b_acc[:, :width],
-                    lhsT=wb_w[u][:, a, n0 : n0 + P].bitcast(FP8X4),
+                    out=b_acc[:],
+                    lhsT=wb_w[i // 2][:, a, n0 : n0 + P].bitcast(FP8X4),
                     lhsT_scale=wb_s[:, a, :].bitcast(U8)[:, i * P : (i + 1) * P],
                     rhs=v_w[a][:, cols].bitcast(FP8X4),
                     rhs_scale=v_s[4 * a :, cols],
                     start=(a == 0),
                     stop=(a == PASSES - 1),
                 )
-            nc.vector.tensor_tensor(new[i][:, cols], b_acc[:, :width], new[i][:, cols], ALU.add)
+            return b_acc
+
+        def add_token(i, half):
+            cols = slice(half * HALF, (half + 1) * HALF)
+            b_acc = token_product(i, half)
+            if (i, half) in ADD_ON_GPSIMD:
+                b_sb = keep.tile([P, HALF], F32, name=f"b_sb{i}")
+                nc.scalar.copy(b_sb[:], b_acc[:])
+                nc.gpsimd.tensor_tensor(new[i][:, cols], b_sb[:], new[i][:, cols], ALU.add)
+            else:
+                nc.vector.tensor_tensor(new[i][:, cols], b_acc[:], new[i][:, cols], ALU.add)
 
         def store(i, j0, width):
             nc.sync.dma_start(out[i * P : (i + 1) * P, j0 : j0 + width], new[i][:, j0 : j0 + width])
 
-        cast_w1(0, 96)
         gather_scales(0, S)
+        cast_w1(0, 96)
         quantize_w1(0)
-        gather_words(0, 0, HALF)
-        gather_words(0, HALF, HALF)
-        cast_w1(1, 64)
+        for q in range(4):
+            gather_words(0, q * QUARTER, QUARTER)
+        cast_w1(1, 80)
         quantize_w1(1)
         for c in range(S // CHUNK):
             hidden_pass(c, 0)
         for q in range(4):
             gather_words(1, q * QUARTER, QUARTER)
-        for q in range(4):
-            for c in (2 * q, 2 * q + 1):
+        for u in range(2):
+            for c in range(4 * u, 4 * u + 4):
                 hidden_pass(c, 1)
-                relu(c, c in (3, 5, 7))
-            quantize_h(q)
-            if q == 1:
-                apply_decay(0, 0, HALF)
-            elif q > 1:
-                apply_decay(0, q * QUARTER, QUARTER)
-
-        apply_decay(1, 0, HALF)
-        apply_decay(1, HALF, HALF)
+                relu(c)
+            quantize_h(u)
 
         def finish(i):
-            add_token(i, 0, HALF)
-            add_token(i, HALF, HALF)
+            add_token(i, 0)
+            add_token(i, 1)
             store(i, 0, S)
 
-        finish(0)
-        for i in range(2, TILES - 1):
-            apply_decay(i, 0, S)
-            if i % 2 == 0:
-                finish(i - 1)
-                finish(i)
         last = TILES - 1
-        apply_decay(last, 0, HALF)
-        apply_decay(last, HALF, QUARTER)
-        add_token(last, 0, HALF)
-        store(last, 0, HALF)
-        apply_decay(last, 3 * QUARTER, QUARTER)
-        for j0 in (HALF, 3 * QUARTER):
-            add_token(last, j0, QUARTER)
-            store(last, j0, QUARTER)
+        gather_state(0)
+        gather_state(1)
+        for half in range(2):
+            apply_decay(0, half * HALF, HALF, 2 * half)
+            apply_decay(1, half * HALF, HALF, 2 * half + 1)
+        for i in range(2, last):
+            gather_state(i)
+            apply_decay(i, 0, S, 0)
+            if i in (3, 5):
+                finish(i - 3)
+                finish(i - 2)
+        gather_state(last)
+        apply_decay(last, 0, HALF, 0)
+        apply_decay(last, HALF, HALF, 1)
+        for i in range(4, TILES):
+            for half in range(2):
+                add_token(i, half)
+                store(i, half * HALF, HALF)

@@ -25,7 +25,7 @@ QUARTER = 256
 HALF = 512
 ROW_GAP = 8
 GATHER_ROWS = ((0, 5), (5, 8))
-ADD_ON_GPSIMD = ((0, 1), (2, 1))
+ADD_ON_GPSIMD = ((0, 1), (1, 1), (2, 1))
 
 
 def tile_list_session_state_decay_kernel(
@@ -41,11 +41,11 @@ def tile_list_session_state_decay_kernel(
         tab_s = keep.tile([P, T // 4], I32, name="tab_s", tag="w1_q0", align_bytes=64)
         wa_s = keep.tile([P, N // 4], I32, name="wa_s", align_bytes=64)
         wb_s = keep.tile([P, PASSES, N // 4], I32, name="wb_s", align_bytes=64)
-        w1_raw = [keep.tile([P, PACK, H], F32, name=f"w1_raw{a}") for a in range(PASSES)]
+        w1_raw = [[keep.tile([P, PACK, H // 2], F32, name=f"w1_raw{a}_{u}") for u in range(2)] for a in range(PASSES)]
         w1_bf = [keep.tile([P, PACK * H], BF16, name=f"w1_bf{a}", align_bytes=64) for a in range(PASSES)]
         w1_s = [keep.tile([P, H], U8, name=f"w1_s{a}", align_bytes=64) for a in range(PASSES)]
         wa_w = keep.tile([P, 2 * N], U8, name="wa_w", align_bytes=64)
-        wb_w = [keep.tile([P, PASSES, 2 * P], I32, name=f"wb_w{u}", align_bytes=64) for u in range(TILES // 2)]
+        wb_w = [keep.tile([P, PASSES, N // 2], I32, name=f"wb_w{u}", align_bytes=64) for u in range(2)]
         state = [keep.tile([P, T], F32, name=f"state{i}") for i in range(TILES)]
         v_w = [keep.tile([P, S], U32, name=f"v_w{a}", align_bytes=64) for a in range(PASSES)]
         v_s = keep.tile([P, S], U8, name="v_s", align_bytes=64)
@@ -61,9 +61,9 @@ def tile_list_session_state_decay_kernel(
 
         wb_view = wb_words.rearrange("a p n i -> p a (n i)")
 
-        def load_w1(a, first, end):
-            rows = w1[a * P * PACK : (a + 1) * P * PACK, :]
-            nc.sync.dma_start(w1_raw[a][:, first:end, :], rows.rearrange("(p j) c -> p j c", j=PACK)[:, first:end, :])
+        def load_w1(a, u):
+            rows = w1[a * P * PACK : (a + 1) * P * PACK, u * H // 2 : (u + 1) * H // 2]
+            nc.sync.dma_start(w1_raw[a][u][:], rows.rearrange("(p j) c -> p j c", j=PACK))
 
         def load_table(a):
             nc.sync.dma_start(tab_w[a][:], tab_words[a].rearrange("p t i -> p (t i)").bitcast(I32))
@@ -76,37 +76,34 @@ def tile_list_session_state_decay_kernel(
             nc.sync.dma_start(state[i][:], gT[i * P : (i + 1) * P, :])
 
         def load_wb(u):
-            nc.sync.dma_start(wb_w[u][:], wb_view[:, :, 2 * u * P * PACK : 2 * (u + 1) * P * PACK].bitcast(I32))
+            nc.sync.dma_start(wb_w[u][:], wb_view[:, :, u * N // 2 * PACK : (u + 1) * N // 2 * PACK].bitcast(I32))
 
         nc.sync.dma_start(offsets[:], offs)
-        load_w1(0, 0, 2)
+        load_w1(0, 0)
         for q in range(4):
             load_table_scales(q, 0, 2)
-        load_w1(0, 2, 4)
+        load_w1(0, 1)
         load_table(0)
         for r in range(4):
             nc.sync.dma_start(wa_s[r:P:32, :], wa_scales[0, r:16:4, :].bitcast(I32))
-        load_w1(1, 0, 4)
+        load_w1(1, 0)
+        load_w1(1, 1)
         load_table(1)
         load_state(0)
         load_state(1)
+        nc.sync.dma_start(wa_w[:].bitcast(I32), wa_words[0].bitcast(I32))
         for r in range(4):
             nc.sync.dma_start(wb_s[r:P:32, :, :], wb_scales[:, r:16:4, :].rearrange("a q n -> q a n").bitcast(I32))
-        nc.sync.dma_start(wa_w[:].bitcast(I32), wa_words[0].bitcast(I32))
-        load_state(2)
-        load_state(3)
         load_wb(0)
-        for u in (1, 2):
-            load_state(2 * u + 2)
-            load_state(2 * u + 3)
-            load_wb(u)
-        load_wb(3)
+        for i in range(2, TILES):
+            load_state(i)
+        load_wb(1)
 
-        def cast_w1(a, split):
+        def cast_w1(a):
             dst = w1_bf[a][:].rearrange("p (t m j) -> p m t j", t=PACK, j=PACK)
-            src = w1_raw[a][:].rearrange("p j (m t) -> p m t j", t=PACK)
-            nc.scalar.activation(dst[:, :split], src[:, :split], ACT.Copy)
-            nc.vector.tensor_copy(dst[:, split:], src[:, split:])
+            for u in range(2):
+                src = w1_raw[a][u][:].rearrange("p j (m t) -> p m t j", t=PACK)
+                nc.scalar.activation(dst[:, u * P // 2 : (u + 1) * P // 2], src, ACT.Copy)
 
         w1_q = {}
 
@@ -189,12 +186,12 @@ def tile_list_session_state_decay_kernel(
 
         def token_product(i, half):
             cols = slice(half * HALF, (half + 1) * HALF)
-            b_acc = psum.tile([P, HALF], F32, name="b_acc", tag=f"bank{2 + (2 * i + half) % 6}")
-            n0 = (i % 2) * P
+            b_acc = psum.tile([P, HALF], F32, name="b_acc", tag=f"bank{2 + (2 * i + half + 2) % 6}")
+            n0 = (i % 4) * P
             for a in range(PASSES):
                 nc.tensor.matmul_mx(
                     out=b_acc[:],
-                    lhsT=wb_w[i // 2][:, a, n0 : n0 + P].bitcast(FP8X4),
+                    lhsT=wb_w[i // 4][:, a, n0 : n0 + P].bitcast(FP8X4),
                     lhsT_scale=wb_s[:, a, :].bitcast(U8)[:, i * P : (i + 1) * P],
                     rhs=v_w[a][:, cols].bitcast(FP8X4),
                     rhs_scale=v_s[4 * a :, cols],
@@ -203,25 +200,27 @@ def tile_list_session_state_decay_kernel(
                 )
             return b_acc
 
-        def add_token(i, half):
+        def add_token(i, half, dst):
             cols = slice(half * HALF, (half + 1) * HALF)
             b_acc = token_product(i, half)
             if (i, half) in ADD_ON_GPSIMD:
                 b_sb = keep.tile([P, HALF], F32, name=f"b_sb{i}")
                 nc.scalar.copy(b_sb[:], b_acc[:])
-                nc.gpsimd.tensor_tensor(new[i][:, cols], b_sb[:], new[i][:, cols], ALU.add)
+                dst = new[i]
+                nc.gpsimd.tensor_tensor(dst[:, cols], b_sb[:], new[i][:, cols], ALU.add)
             else:
-                nc.vector.tensor_tensor(new[i][:, cols], b_acc[:], new[i][:, cols], ALU.add)
+                nc.vector.tensor_tensor(dst[:, cols], b_acc[:], new[i][:, cols], ALU.add)
+            nc.sync.dma_start(out[i * P : (i + 1) * P, cols], dst[:, cols])
 
         def store(i, j0, width):
             nc.sync.dma_start(out[i * P : (i + 1) * P, j0 : j0 + width], new[i][:, j0 : j0 + width])
 
         gather_scales(0, S)
-        cast_w1(0, 96)
+        cast_w1(0)
         quantize_w1(0)
         for q in range(4):
             gather_words(0, q * QUARTER, QUARTER)
-        cast_w1(1, 80)
+        cast_w1(1)
         quantize_w1(1)
         for c in range(S // CHUNK):
             hidden_pass(c, 0)
@@ -233,10 +232,11 @@ def tile_list_session_state_decay_kernel(
                 relu(c)
             quantize_h(u)
 
-        def finish(i):
-            add_token(i, 0)
-            add_token(i, 1)
-            store(i, 0, S)
+        def finish_pair(i, freed):
+            result = keep.tile([P, 2, S], F32, name=f"result{i}", tag=f"state{freed}")
+            for u in range(2):
+                for half in range(2):
+                    add_token(i + u, half, result[:, u, :])
 
         last = TILES - 1
         gather_state(0)
@@ -248,12 +248,16 @@ def tile_list_session_state_decay_kernel(
             gather_state(i)
             apply_decay(i, 0, S, 0)
             if i in (3, 5):
-                finish(i - 3)
-                finish(i - 2)
+                finish_pair(i - 3, i)
         gather_state(last)
         apply_decay(last, 0, HALF, 0)
         apply_decay(last, HALF, HALF, 1)
-        for i in range(4, TILES):
+        for i in range(4, last):
             for half in range(2):
-                add_token(i, half)
-                store(i, half * HALF, HALF)
+                add_token(i, half, new[i])
+        add_token(last, 0, new[last])
+        b_acc = token_product(last, 1)
+        for j0 in (HALF, 3 * QUARTER):
+            cols = slice(j0, j0 + QUARTER)
+            nc.vector.tensor_tensor(new[last][:, cols], b_acc[:, j0 - HALF : j0 - HALF + QUARTER], new[last][:, cols], ALU.add)
+            store(last, j0, QUARTER)

@@ -41,7 +41,8 @@ def tile_list_session_state_decay_kernel(
         tab_s = keep.tile([P, T // 4], I32, name="tab_s", tag="w1_q0", align_bytes=64)
         wa_s = keep.tile([P, N // 4], I32, name="wa_s", align_bytes=64)
         wb_s = keep.tile([P, PASSES, N // 4], I32, name="wb_s", align_bytes=64)
-        w1_raw = [[keep.tile([P, PACK, H // 2], F32, name=f"w1_raw{a}_{u}") for u in range(2)] for a in range(PASSES)]
+        w1_raw = [keep.tile([P, PACK, H], F32, name=f"w1_raw{a}") for a in range(PASSES)]
+        warm = keep.tile([P, 8], F32, name="warm")
         w1_bf = [keep.tile([P, PACK * H], BF16, name=f"w1_bf{a}", align_bytes=64) for a in range(PASSES)]
         w1_s = [keep.tile([P, H], U8, name=f"w1_s{a}", align_bytes=64) for a in range(PASSES)]
         wa_w = keep.tile([P, 2 * N], U8, name="wa_w", align_bytes=64)
@@ -59,11 +60,14 @@ def tile_list_session_state_decay_kernel(
         for plane in (tab_s, wa_s, wb_s):
             nc.vector.memset(plane[:], 0)
 
+        nc.gpsimd.memset(warm[:, :1], 0.0)
+        nc.scalar.activation(warm[:, 4:5], warm[:, :1], ACT.Exp)
+
         wb_view = wb_words.rearrange("a p n i -> p a (n i)")
 
-        def load_w1(a, u):
-            rows = w1[a * P * PACK : (a + 1) * P * PACK, u * H // 2 : (u + 1) * H // 2]
-            nc.sync.dma_start(w1_raw[a][u][:], rows.rearrange("(p j) c -> p j c", j=PACK))
+        def load_w1(a, first, end):
+            rows = w1[a * P * PACK : (a + 1) * P * PACK, :]
+            nc.sync.dma_start(w1_raw[a][:, first:end, :], rows.rearrange("(p j) c -> p j c", j=PACK)[:, first:end, :])
 
         def load_table(a):
             nc.sync.dma_start(tab_w[a][:], tab_words[a].rearrange("p t i -> p (t i)").bitcast(I32))
@@ -79,15 +83,14 @@ def tile_list_session_state_decay_kernel(
             nc.sync.dma_start(wb_w[u][:], wb_view[:, :, u * N // 2 * PACK : (u + 1) * N // 2 * PACK].bitcast(I32))
 
         nc.sync.dma_start(offsets[:], offs)
-        load_w1(0, 0)
+        load_w1(0, 0, 2)
         for q in range(4):
             load_table_scales(q, 0, 2)
-        load_w1(0, 1)
+        load_w1(0, 2, 4)
         load_table(0)
         for r in range(4):
             nc.sync.dma_start(wa_s[r:P:32, :], wa_scales[0, r:16:4, :].bitcast(I32))
-        load_w1(1, 0)
-        load_w1(1, 1)
+        load_w1(1, 0, 4)
         load_table(1)
         load_state(0)
         load_state(1)
@@ -99,11 +102,11 @@ def tile_list_session_state_decay_kernel(
             load_state(i)
         load_wb(1)
 
-        def cast_w1(a):
+        def cast_w1(a, split):
             dst = w1_bf[a][:].rearrange("p (t m j) -> p m t j", t=PACK, j=PACK)
-            for u in range(2):
-                src = w1_raw[a][u][:].rearrange("p j (m t) -> p m t j", t=PACK)
-                nc.scalar.activation(dst[:, u * P // 2 : (u + 1) * P // 2], src, ACT.Copy)
+            src = w1_raw[a][:].rearrange("p j (m t) -> p m t j", t=PACK)
+            nc.scalar.activation(dst[:, :split], src[:, :split], ACT.Copy)
+            nc.vector.tensor_copy(dst[:, split:], src[:, split:])
 
         w1_q = {}
 
@@ -216,11 +219,11 @@ def tile_list_session_state_decay_kernel(
             nc.sync.dma_start(out[i * P : (i + 1) * P, j0 : j0 + width], new[i][:, j0 : j0 + width])
 
         gather_scales(0, S)
-        cast_w1(0)
+        cast_w1(0, 96)
         quantize_w1(0)
         for q in range(4):
             gather_words(0, q * QUARTER, QUARTER)
-        cast_w1(1)
+        cast_w1(1, 72)
         quantize_w1(1)
         for c in range(S // CHUNK):
             hidden_pass(c, 0)

@@ -82,8 +82,8 @@ def tile_list_session_state_decay_kernel(
         def load_wb(u):
             nc.sync.dma_start(wb_w[u][:], wb_view[:, :, u * N // 2 * PACK : (u + 1) * N // 2 * PACK].bitcast(I32))
 
-        nc.sync.dma_start(offsets[:], offs)
         load_w1(0, 0, 2)
+        nc.sync.dma_start(offsets[:], offs)
         for q in range(4):
             load_table_scales(q, 0, 2)
         load_w1(0, 2, 4)
@@ -156,7 +156,7 @@ def tile_list_session_state_decay_kernel(
             picked[i] = keep.tile(
                 [P, S // CHUNK, CHUNK + ROW_GAP], U32, name=f"picked{i}", tag=f"stage{i % 4}", align_bytes=64
             )
-            for first, end in GATHER_ROWS:
+            for first, end in GATHER_ROWS if i else ((0, 4), (4, 8)):
                 nc.vector.tensor_copy(
                     picked[i][:, first:end, :CHUNK],
                     state[i][:].bitcast(U32).indirect(listed(first * CHUNK, (end - first) * CHUNK)),
@@ -212,7 +212,7 @@ def tile_list_session_state_decay_kernel(
                 dst = new[i]
                 nc.gpsimd.tensor_tensor(dst[:, cols], b_sb[:], new[i][:, cols], ALU.add)
             else:
-                nc.vector.tensor_tensor(dst[:, cols], b_acc[:], new[i][:, cols], ALU.add)
+                nc.vector.tensor_tensor(dst[:, cols], new[i][:, cols], b_acc[:], ALU.add)
             nc.sync.dma_start(out[i * P : (i + 1) * P, cols], dst[:, cols])
 
         def store(i, j0, width):
@@ -262,5 +262,5 @@ def tile_list_session_state_decay_kernel(
         b_acc = token_product(last, 1)
         for j0 in (HALF, 3 * QUARTER):
             cols = slice(j0, j0 + QUARTER)
-            nc.vector.tensor_tensor(new[last][:, cols], b_acc[:, j0 - HALF : j0 - HALF + QUARTER], new[last][:, cols], ALU.add)
+            nc.vector.tensor_tensor(new[last][:, cols], new[last][:, cols], b_acc[:, j0 - HALF : j0 - HALF + QUARTER], ALU.add)
             store(last, j0, QUARTER)

@@ -88,18 +88,22 @@ def tile_list_session_state_decay_kernel(
             load_table_scales(q, 0, 2)
         load_w1(0, 2, 4)
         load_table(0)
-        for r in range(4):
-            nc.sync.dma_start(wa_s[r:P:32, :], wa_scales[0, r:16:4, :].bitcast(I32))
         load_w1(1, 0, 4)
         load_table(1)
         load_state(0)
         load_state(1)
+        for r in range(4):
+            nc.sync.dma_start(wa_s[r:P:32, :], wa_scales[0, r:16:4, :].bitcast(I32))
         nc.sync.dma_start(wa_w[:].bitcast(I32), wa_words[0].bitcast(I32))
+        load_wb(0)
         for r in range(4):
             nc.sync.dma_start(wb_s[r:P:32, :, :], wb_scales[:, r:16:4, :].rearrange("a q n -> q a n").bitcast(I32))
-        load_wb(0)
-        for i in range(2, TILES):
-            load_state(i)
+        load_state(2)
+        load_state(3)
+        load_state(4)
+        load_state(5)
+        load_state(6)
+        load_state(7)
         load_wb(1)
 
         def cast_w1(a, split):

@@ -38,7 +38,7 @@ def tile_list_session_state_decay_kernel(
 
         offsets = keep.tile([P, S // 16], U16, name="offsets")
         tab_w = [keep.tile([P, T], I32, name=f"tab_w{a}", align_bytes=64) for a in range(PASSES)]
-        tab_s = keep.tile([P, T // 4], I32, name="tab_s", tag="w1_q0", align_bytes=64)
+        tab_s = keep.tile([P, T // 4], I32, name="tab_s", align_bytes=64)
         wa_s = keep.tile([P, N // 4], I32, name="wa_s", align_bytes=64)
         wb_s = keep.tile([P, PASSES, N // 4], I32, name="wb_s", align_bytes=64)
         w1_raw = [keep.tile([P, PACK, H], F32, name=f"w1_raw{a}") for a in range(PASSES)]
@@ -49,7 +49,8 @@ def tile_list_session_state_decay_kernel(
         wb_w = [keep.tile([P, PASSES, N // 2], I32, name=f"wb_w{u}", align_bytes=64) for u in range(2)]
         state = [keep.tile([P, T], F32, name=f"state{i}") for i in range(TILES)]
         v_w = [keep.tile([P, S], U32, name=f"v_w{a}", align_bytes=64) for a in range(PASSES)]
-        v_s = keep.tile([P, S], U8, name="v_s", align_bytes=64)
+        v_rows = keep.tile([P, S], U8, name="v_rows", align_bytes=64)
+        v_s = [keep.tile([P, S // 4], I32, name=f"v_s{a}", align_bytes=64) for a in range(PASSES)]
         h_q = keep.tile([P, S], U32, name="h_q", align_bytes=64)
         h_s = keep.tile([P, S], U8, name="h_s", align_bytes=64)
         h_bf = [
@@ -57,7 +58,9 @@ def tile_list_session_state_decay_kernel(
         ]
         new = [keep.tile([P, S], F32, name=f"new{i}") for i in range(TILES)]
 
-        for plane in (tab_s, wa_s, wb_s):
+        nc.vector.memset(tab_s[32:64, :], 0)
+        nc.vector.memset(tab_s[64:, :], 0)
+        for plane in (v_s[0], v_s[1], wa_s, wb_s):
             nc.vector.memset(plane[:], 0)
 
         nc.gpsimd.memset(warm[:, :1], 0.0)
@@ -72,9 +75,9 @@ def tile_list_session_state_decay_kernel(
         def load_table(a):
             nc.sync.dma_start(tab_w[a][:], tab_words[a].rearrange("p t i -> p (t i)").bitcast(I32))
 
-        def load_table_scales(q, first, end):
-            rows = tab_scales[first:end, 4 * q : 4 * q + 4, :]
-            nc.sync.dma_start(tab_s[32 * q + 4 * first : 32 * q + 4 * end, :], rows.bitcast(I32))
+        def place_scales(a, r):
+            rows = v_rows[:].bitcast(I32)[16 * a + r : 16 * a + 16 : 4, :]
+            nc.sync.dma_start(v_s[a][r:P:32, :], rows)
 
         def load_state(i):
             nc.sync.dma_start(state[i][:], gT[i * P : (i + 1) * P, :])
@@ -82,14 +85,17 @@ def tile_list_session_state_decay_kernel(
         def load_wb(u):
             nc.sync.dma_start(wb_w[u][:], wb_view[:, :, u * N // 2 * PACK : (u + 1) * N // 2 * PACK].bitcast(I32))
 
-        load_w1(0, 0, 2)
         nc.sync.dma_start(offsets[:], offs)
-        for q in range(4):
-            load_table_scales(q, 0, 2)
-        load_w1(0, 2, 4)
+        nc.sync.dma_start(tab_s[:32, :], tab_scales.rearrange("a q t -> (a q) t").bitcast(I32))
         load_table(0)
+        load_w1(0, 0, 4)
         load_w1(1, 0, 4)
+        nc.vector.tensor_copy(v_rows[:], tab_s[:].bitcast(U8).indirect(offsets[:]))
+        for r in range(4):
+            place_scales(0, r)
         load_table(1)
+        for r in range(4):
+            place_scales(1, r)
         load_state(0)
         load_state(1)
         for r in range(4):
@@ -124,9 +130,6 @@ def tile_list_session_state_decay_kernel(
         def gather_words(a, j0, width):
             nc.vector.tensor_copy(v_w[a][:, j0 : j0 + width], tab_w[a][:].bitcast(U32).indirect(listed(j0, width)))
 
-        def gather_scales(j0, width):
-            nc.vector.tensor_copy(v_s[:, j0 : j0 + width], tab_s[:].bitcast(U8).indirect(listed(j0, width)))
-
         h_acc = [psum.tile([P, PACK, CHUNK], F32, name=f"h_acc{c}", tag=f"bank{c}") for c in range(S // CHUNK)]
 
         def hidden_pass(c, a):
@@ -138,7 +141,7 @@ def tile_list_session_state_decay_kernel(
                     lhsT=w1_q[a][:, r].bitcast(FP8X4),
                     lhsT_scale=w1_s[a][:, r],
                     rhs=v_w[a][:, cols].bitcast(FP8X4),
-                    rhs_scale=v_s[4 * a :, cols],
+                    rhs_scale=v_s[a][:].bitcast(U8)[:, cols],
                     start=(a == 0 and t == 0),
                     stop=(a == PASSES - 1 and t == PACK - 1),
                 )
@@ -201,7 +204,7 @@ def tile_list_session_state_decay_kernel(
                     lhsT=wb_w[i // 4][:, a, n0 : n0 + P].bitcast(FP8X4),
                     lhsT_scale=wb_s[:, a, :].bitcast(U8)[:, i * P : (i + 1) * P],
                     rhs=v_w[a][:, cols].bitcast(FP8X4),
-                    rhs_scale=v_s[4 * a :, cols],
+                    rhs_scale=v_s[a][:].bitcast(U8)[:, cols],
                     start=(a == 0),
                     stop=(a == PASSES - 1),
                 )
@@ -222,12 +225,10 @@ def tile_list_session_state_decay_kernel(
         def store(i, j0, width):
             nc.sync.dma_start(out[i * P : (i + 1) * P, j0 : j0 + width], new[i][:, j0 : j0 + width])
 
-        gather_scales(0, S)
-        cast_w1(0, 96)
+        gather_words(0, 0, S)
+        cast_w1(0, 64)
         quantize_w1(0)
-        for q in range(4):
-            gather_words(0, q * QUARTER, QUARTER)
-        cast_w1(1, 72)
+        cast_w1(1, 64)
         quantize_w1(1)
         for c in range(S // CHUNK):
             hidden_pass(c, 0)

@@ -21,11 +21,14 @@ PACK = 4
 PASSES = K // (P * PACK)
 TILES = N // P
 CHUNK = 128
+ROWS = S // CHUNK
 QUARTER = 256
 HALF = 512
 ROW_GAP = 8
+GPSIMD_HALVES = 3
 GATHER_ROWS = ((0, 5), (5, 8))
-ADD_ON_GPSIMD = ((0, 1), (1, 1), (2, 1))
+WB_CUTS = ((0, 2), (2, 3), (3, 4), (4, 8))
+WB_BEHIND_STATE = (1, 5, 6, 7)
 
 
 def tile_list_session_state_decay_kernel(
@@ -46,7 +49,9 @@ def tile_list_session_state_decay_kernel(
         w1_bf = [keep.tile([P, PACK * H], BF16, name=f"w1_bf{a}", align_bytes=64) for a in range(PASSES)]
         w1_s = [keep.tile([P, H], U8, name=f"w1_s{a}", align_bytes=64) for a in range(PASSES)]
         wa_w = keep.tile([P, 2 * N], U8, name="wa_w", align_bytes=64)
-        wb_w = [keep.tile([P, PASSES, N // 2], I32, name=f"wb_w{u}", align_bytes=64) for u in range(2)]
+        wb_w = [
+            keep.tile([P, PASSES, (end - first) * P], I32, name=f"wb_w{first}", align_bytes=64) for first, end in WB_CUTS
+        ]
         state = [keep.tile([P, T], F32, name=f"state{i}") for i in range(TILES)]
         v_w = [keep.tile([P, S], U32, name=f"v_w{a}", align_bytes=64) for a in range(PASSES)]
         v_rows = keep.tile([P, S], U8, name="v_rows", align_bytes=64)
@@ -54,9 +59,10 @@ def tile_list_session_state_decay_kernel(
         h_q = keep.tile([P, S], U32, name="h_q", align_bytes=64)
         h_s = keep.tile([P, S], U8, name="h_s", align_bytes=64)
         h_bf = [
-            keep.tile([P, 4, CHUNK * PACK], BF16, name=f"h_bf{u}", tag=f"stage{u + 2}", align_bytes=64) for u in range(2)
+            keep.tile([P, 4, CHUNK * PACK], BF16, name=f"h_bf{u}", tag=f"h_bf{u}", align_bytes=64) for u in range(2)
         ]
-        new = [keep.tile([P, S], F32, name=f"new{i}") for i in range(TILES)]
+        new_pair = keep.tile([P, 2, S], F32, name="new_pair")
+        new = [new_pair[:, i, :] if i < 2 else keep.tile([P, S], F32, name=f"new{i}", tag=f"new{i}")[:] for i in range(TILES)]
 
         nc.vector.memset(tab_s[32:64, :], 0)
         nc.vector.memset(tab_s[64:, :], 0)
@@ -83,7 +89,11 @@ def tile_list_session_state_decay_kernel(
             nc.sync.dma_start(state[i][:], gT[i * P : (i + 1) * P, :])
 
         def load_wb(u):
-            nc.sync.dma_start(wb_w[u][:], wb_view[:, :, u * N // 2 * PACK : (u + 1) * N // 2 * PACK].bitcast(I32))
+            first, end = WB_CUTS[u]
+            nc.sync.dma_start(wb_w[u][:], wb_view[:, :, first * P * PACK : end * P * PACK].bitcast(I32))
+
+        def load_wb_scales(r):
+            nc.sync.dma_start(wb_s[r:P:32, :, :], wb_scales[:, r:16:4, :].rearrange("a q n -> q a n").bitcast(I32))
 
         nc.sync.dma_start(offsets[:], offs)
         nc.sync.dma_start(tab_s[:32, :], tab_scales.rearrange("a q t -> (a q) t").bitcast(I32))
@@ -97,20 +107,19 @@ def tile_list_session_state_decay_kernel(
         for r in range(4):
             place_scales(1, r)
         load_state(0)
-        load_state(1)
         for r in range(4):
             nc.sync.dma_start(wa_s[r:P:32, :], wa_scales[0, r:16:4, :].bitcast(I32))
         nc.sync.dma_start(wa_w[:].bitcast(I32), wa_words[0].bitcast(I32))
+        load_state(1)
         load_wb(0)
-        for r in range(4):
-            nc.sync.dma_start(wb_s[r:P:32, :, :], wb_scales[:, r:16:4, :].rearrange("a q n -> q a n").bitcast(I32))
+        for r in range(3):
+            load_wb_scales(r)
         load_state(2)
-        load_state(3)
-        load_state(4)
-        load_state(5)
-        load_state(6)
-        load_state(7)
-        load_wb(1)
+        load_wb_scales(3)
+        for i in range(3, TILES):
+            load_state(i)
+            if i in WB_BEHIND_STATE:
+                load_wb(WB_BEHIND_STATE.index(i))
 
         def cast_w1(a, split):
             dst = w1_bf[a][:].rearrange("p (t m j) -> p m t j", t=PACK, j=PACK)
@@ -130,7 +139,10 @@ def tile_list_session_state_decay_kernel(
         def gather_words(a, j0, width):
             nc.vector.tensor_copy(v_w[a][:, j0 : j0 + width], tab_w[a][:].bitcast(U32).indirect(listed(j0, width)))
 
-        h_acc = [psum.tile([P, PACK, CHUNK], F32, name=f"h_acc{c}", tag=f"bank{c}") for c in range(S // CHUNK)]
+        h_acc = {}
+
+        def open_chunk(c):
+            h_acc[c] = psum.tile([P, PACK, CHUNK], F32, name=f"h_acc{c}", tag=f"bank{c % 4}")
 
         def hidden_pass(c, a):
             cols = slice(c * CHUNK, (c + 1) * CHUNK)
@@ -157,51 +169,48 @@ def tile_list_session_state_decay_kernel(
                 out=h_q[:, cols].bitcast(FP8X4), scales=h_s[:, cols], in_=h_bf[q][:].rearrange("p c w -> p (c w)")
             )
 
-        picked = {}
+        def picked_tile(name, rows, tag):
+            return keep.tile([P, rows, CHUNK + ROW_GAP], U32, name=name, tag=tag, align_bytes=64)
 
-        def gather_state(i):
-            picked[i] = keep.tile(
-                [P, S // CHUNK, CHUNK + ROW_GAP], U32, name=f"picked{i}", tag=f"stage{i % 4}", align_bytes=64
-            )
-            for first, end in GATHER_ROWS if i else ((0, 4), (4, 8)):
-                nc.vector.tensor_copy(
-                    picked[i][:, first:end, :CHUNK],
-                    state[i][:].bitcast(U32).indirect(listed(first * CHUNK, (end - first) * CHUNK)),
-                )
-
-        def apply_decay(i, j0, width, bank):
-            decay = new[i][:, j0 : j0 + width]
-            for c0 in range(0, width, HALF):
-                n = min(HALF, width - c0)
-                cols = slice(j0 + c0, j0 + c0 + n)
-                a_acc = psum.tile([P, HALF], F32, name="a_acc", tag=f"bank{bank + c0 // HALF}")
-                nc.tensor.matmul_mx(
-                    out=a_acc[:, :n],
-                    lhsT=wa_w[:, 2 * i * P : 2 * (i + 1) * P].bitcast(FP4X4),
-                    lhsT_scale=wa_s[:].bitcast(U8)[:, i * P : (i + 1) * P],
-                    rhs=h_q[:, cols].bitcast(FP8X4),
-                    rhs_scale=h_s[:, cols],
-                    start=True,
-                    stop=True,
-                )
-                nc.scalar.activation(decay[:, c0 : c0 + n], a_acc[:, :n], ACT.Exp)
-            nc.scalar.activation(decay, decay, ACT.Exp, scale=-1.0)
-            rows = slice(j0 // CHUNK, (j0 + width) // CHUNK)
-            nc.gpsimd.tensor_tensor(
-                decay.rearrange("p (r c) -> p r c", c=CHUNK),
-                picked[i][:, rows, :CHUNK].bitcast(F32),
-                decay.rearrange("p (r c) -> p r c", c=CHUNK),
-                ALU.mult,
+        def gather_rows(dst, i, first, end):
+            nc.vector.tensor_copy(
+                dst[:, :, :CHUNK], state[i][:].bitcast(U32).indirect(listed(first * CHUNK, (end - first) * CHUNK))
             )
 
-        def token_product(i, half):
+        def gather_state(i, picked):
+            for first, end in GATHER_ROWS:
+                gather_rows(picked[:, first:end, :], i, first, end)
+
+        def rate(i, half, bank):
             cols = slice(half * HALF, (half + 1) * HALF)
-            b_acc = psum.tile([P, HALF], F32, name="b_acc", tag=f"bank{2 + (2 * i + half + 2) % 6}")
-            n0 = (i % 4) * P
+            a_acc = psum.tile([P, HALF], F32, name="a_acc", tag=f"bank{bank}")
+            nc.tensor.matmul_mx(
+                out=a_acc[:],
+                lhsT=wa_w[:, 2 * i * P : 2 * (i + 1) * P].bitcast(FP4X4),
+                lhsT_scale=wa_s[:].bitcast(U8)[:, i * P : (i + 1) * P],
+                rhs=h_q[:, cols].bitcast(FP8X4),
+                rhs_scale=h_s[:, cols],
+                start=True,
+                stop=True,
+            )
+            nc.scalar.activation(new[i][:, cols], a_acc[:], ACT.Exp)
+
+        def decay(ap):
+            nc.scalar.activation(ap, ap, ACT.Exp, scale=-1.0)
+
+        def times_state(ap, picked):
+            rows = ap.rearrange("p (r c) -> p r c", c=CHUNK)
+            nc.gpsimd.tensor_tensor(rows, picked[:, :, :CHUNK].bitcast(F32), rows, ALU.mult)
+
+        def token_product(i, half, bank):
+            cols = slice(half * HALF, (half + 1) * HALF)
+            b_acc = psum.tile([P, HALF], F32, name="b_acc", tag=f"bank{bank}")
+            u = [first <= i < end for first, end in WB_CUTS].index(True)
+            n0 = (i - WB_CUTS[u][0]) * P
             for a in range(PASSES):
                 nc.tensor.matmul_mx(
                     out=b_acc[:],
-                    lhsT=wb_w[i // 4][:, a, n0 : n0 + P].bitcast(FP8X4),
+                    lhsT=wb_w[u][:, a, n0 : n0 + P].bitcast(FP8X4),
                     lhsT_scale=wb_s[:, a, :].bitcast(U8)[:, i * P : (i + 1) * P],
                     rhs=v_w[a][:, cols].bitcast(FP8X4),
                     rhs_scale=v_s[a][:].bitcast(U8)[:, cols],
@@ -210,62 +219,73 @@ def tile_list_session_state_decay_kernel(
                 )
             return b_acc
 
-        def add_token(i, half, dst):
-            cols = slice(half * HALF, (half + 1) * HALF)
-            b_acc = token_product(i, half)
-            if (i, half) in ADD_ON_GPSIMD:
-                b_sb = keep.tile([P, HALF], F32, name=f"b_sb{i}")
-                nc.scalar.copy(b_sb[:], b_acc[:])
-                dst = new[i]
-                nc.gpsimd.tensor_tensor(dst[:, cols], b_sb[:], new[i][:, cols], ALU.add)
-            else:
-                nc.vector.tensor_tensor(dst[:, cols], new[i][:, cols], b_acc[:], ALU.add)
-            nc.sync.dma_start(out[i * P : (i + 1) * P, cols], dst[:, cols])
+        def store(i, j0, src):
+            nc.sync.dma_start(out[i * P : (i + 1) * P, j0 : j0 + src.shape[1]], src)
 
-        def store(i, j0, width):
-            nc.sync.dma_start(out[i * P : (i + 1) * P, j0 : j0 + width], new[i][:, j0 : j0 + width])
+        def add_on_vector(i, j0, b_acc, dst):
+            nc.vector.tensor_tensor(dst, new[i][:, j0 : j0 + dst.shape[1]], b_acc, ALU.add)
+            store(i, j0, dst)
 
         gather_words(0, 0, S)
         cast_w1(0, 64)
         quantize_w1(0)
         cast_w1(1, 64)
         quantize_w1(1)
-        for c in range(S // CHUNK):
+        for c in range(4):
+            open_chunk(c)
             hidden_pass(c, 0)
         for q in range(4):
             gather_words(1, q * QUARTER, QUARTER)
-        for u in range(2):
-            for c in range(4 * u, 4 * u + 4):
-                hidden_pass(c, 1)
-                relu(c)
-            quantize_h(u)
+        for c in range(4):
+            hidden_pass(c, 1)
+            relu(c)
+        quantize_h(0)
+        for c in range(4, ROWS):
+            open_chunk(c)
+            for a in range(PASSES):
+                hidden_pass(c, a)
+            relu(c)
+        quantize_h(1)
+        picked = picked_tile("picked_pair", 2 * ROWS, "picked_pair")[:].rearrange("p (i r) c -> p i r c", i=2)
+        for i in range(2):
+            gather_state(i, picked[:, i])
+        for i in range(2):
+            rate(i, 0, 4 - 4 * i)
+        for i in range(2):
+            decay(new[i][:, :HALF])
+            times_state(new[i][:, :HALF], picked[:, i, : ROWS // 2, :])
+        for i in range(2):
+            rate(i, 1, 1 + i)
+        decay(new_pair[:, :, HALF:])
+        rows = new_pair[:, :, HALF:].rearrange("p i (r c) -> p i r c", c=CHUNK)
+        nc.gpsimd.tensor_tensor(rows, picked[:, :, ROWS // 2 :, :CHUNK].bitcast(F32), rows, ALU.mult)
 
-        def finish_pair(i, freed):
-            result = keep.tile([P, 2, S], F32, name=f"result{i}", tag=f"state{freed}")
-            for u in range(2):
-                for half in range(2):
-                    add_token(i + u, half, result[:, u, :])
-
+        b_sb = keep.tile([P, GPSIMD_HALVES * HALF], F32, name="b_sb")
+        for k in range(GPSIMD_HALVES):
+            nc.scalar.copy(b_sb[:, k * HALF : (k + 1) * HALF], token_product(k // 2, k % 2, 5 + k)[:])
+        summed = new_pair[:].rearrange("p i s -> p (i s)")[:, : GPSIMD_HALVES * HALF]
+        nc.gpsimd.tensor_tensor(summed, b_sb[:], summed, ALU.add)
+        store(0, 0, new[0])
+        store(1, 0, new[1][:, :HALF])
         last = TILES - 1
-        gather_state(0)
-        gather_state(1)
-        for half in range(2):
-            apply_decay(0, half * HALF, HALF, 2 * half)
-            apply_decay(1, half * HALF, HALF, 2 * half + 1)
-        for i in range(2, last):
-            gather_state(i)
-            apply_decay(i, 0, S, 0)
-            if i in (3, 5):
-                finish_pair(i - 3, i)
-        gather_state(last)
-        apply_decay(last, 0, HALF, 0)
-        apply_decay(last, HALF, HALF, 1)
-        for i in range(4, last):
+        for i in range(2, TILES):
+            picked = picked_tile(f"picked{i}", ROWS, f"picked{i % 4}")
+            gather_state(i, picked)
             for half in range(2):
-                add_token(i, half, new[i])
-        add_token(last, 0, new[last])
-        b_acc = token_product(last, 1)
+                rate(i, half, 5 + half if i == 2 else 7 - 2 * half)
+            if i < last:
+                decay(new[i])
+                times_state(new[i], picked)
+            else:
+                for half in range(2):
+                    cols = slice(half * HALF, (half + 1) * HALF)
+                    decay(new[i][:, cols])
+                    times_state(new[i][:, cols], picked[:, half * ROWS // 2 : (half + 1) * ROWS // 2, :])
+            if i == 2:
+                add_on_vector(1, HALF, token_product(1, 1, 6)[:], new[1][:, HALF:])
+        halves = [(i, half) for i in range(2, TILES) for half in range(2)]
+        for k, (i, half) in enumerate(halves[:-1]):
+            add_on_vector(i, half * HALF, token_product(i, half, k % 5)[:], new[i][:, half * HALF : (half + 1) * HALF])
+        b_acc = token_product(last, 1, (len(halves) - 1) % 5)
         for j0 in (HALF, 3 * QUARTER):
-            cols = slice(j0, j0 + QUARTER)
-            nc.vector.tensor_tensor(new[last][:, cols], new[last][:, cols], b_acc[:, j0 - HALF : j0 - HALF + QUARTER], ALU.add)
-            store(last, j0, QUARTER)
+            add_on_vector(last, j0, b_acc[:, j0 - HALF : j0 - HALF + QUARTER], new[last][:, j0 : j0 + QUARTER])

@@ -25,9 +25,11 @@ ROWS = S // CHUNK
 QUARTER = 256
 HALF = 512
 ROW_GAP = 8
-GPSIMD_HALVES = 3
+SHARED_TILE = 2
+GPSIMD_SHARE = 256
 GATHER_ROWS = ((0, 5), (5, 8))
-WB_CUTS = ((0, 2), (2, 3), (3, 4), (4, 8))
+WA_CUTS = ((0, 2), (2, 8))
+WB_CUTS = ((0, 2), (2, 3), (3, 5), (5, 8))
 WB_BEHIND_STATE = (1, 5, 6, 7)
 
 
@@ -48,7 +50,9 @@ def tile_list_session_state_decay_kernel(
         warm = keep.tile([P, 8], F32, name="warm")
         w1_bf = [keep.tile([P, PACK * H], BF16, name=f"w1_bf{a}", align_bytes=64) for a in range(PASSES)]
         w1_s = [keep.tile([P, H], U8, name=f"w1_s{a}", align_bytes=64) for a in range(PASSES)]
-        wa_w = keep.tile([P, 2 * N], U8, name="wa_w", align_bytes=64)
+        wa_w = [
+            keep.tile([P, 2 * (end - first) * P], U8, name=f"wa_w{first}", align_bytes=64) for first, end in WA_CUTS
+        ]
         wb_w = [
             keep.tile([P, PASSES, (end - first) * P], I32, name=f"wb_w{first}", align_bytes=64) for first, end in WB_CUTS
         ]
@@ -92,6 +96,13 @@ def tile_list_session_state_decay_kernel(
             first, end = WB_CUTS[u]
             nc.sync.dma_start(wb_w[u][:], wb_view[:, :, first * P * PACK : end * P * PACK].bitcast(I32))
 
+        def load_wa(u):
+            first, end = WA_CUTS[u]
+            nc.sync.dma_start(wa_w[u][:].bitcast(I32), wa_words[0][:, 2 * first * P : 2 * end * P].bitcast(I32))
+
+        def load_wa_scales(r):
+            nc.sync.dma_start(wa_s[r:P:32, :], wa_scales[0, r:16:4, :].bitcast(I32))
+
         def load_wb_scales(r):
             nc.sync.dma_start(wb_s[r:P:32, :, :], wb_scales[:, r:16:4, :].rearrange("a q n -> q a n").bitcast(I32))
 
@@ -101,23 +112,27 @@ def tile_list_session_state_decay_kernel(
         load_w1(0, 0, 4)
         load_w1(1, 0, 4)
         nc.vector.tensor_copy(v_rows[:], tab_s[:].bitcast(U8).indirect(offsets[:]))
+        for r in range(2):
+            load_wa_scales(r)
         for r in range(4):
             place_scales(0, r)
         load_table(1)
+        for r in range(2):
+            load_wb_scales(r)
         for r in range(4):
             place_scales(1, r)
         load_state(0)
-        for r in range(4):
-            nc.sync.dma_start(wa_s[r:P:32, :], wa_scales[0, r:16:4, :].bitcast(I32))
-        nc.sync.dma_start(wa_w[:].bitcast(I32), wa_words[0].bitcast(I32))
         load_state(1)
-        load_wb(0)
-        for r in range(3):
-            load_wb_scales(r)
-        load_state(2)
+        for r in range(2, 4):
+            load_wa_scales(r)
+        load_wb_scales(2)
+        load_wa(0)
         load_wb_scales(3)
-        for i in range(3, TILES):
+        load_wb(0)
+        for i in range(2, TILES):
             load_state(i)
+            if i == 3:
+                load_wa(1)
             if i in WB_BEHIND_STATE:
                 load_wb(WB_BEHIND_STATE.index(i))
 
@@ -141,8 +156,8 @@ def tile_list_session_state_decay_kernel(
 
         h_acc = {}
 
-        def open_chunk(c):
-            h_acc[c] = psum.tile([P, PACK, CHUNK], F32, name=f"h_acc{c}", tag=f"bank{c % 4}")
+        def open_chunk(c, bank):
+            h_acc[c] = psum.tile([P, PACK, CHUNK], F32, name=f"h_acc{c}", tag=f"bank{bank}")
 
         def hidden_pass(c, a):
             cols = slice(c * CHUNK, (c + 1) * CHUNK)
@@ -183,10 +198,12 @@ def tile_list_session_state_decay_kernel(
 
         def rate(i, half, bank):
             cols = slice(half * HALF, (half + 1) * HALF)
+            u = [first <= i < end for first, end in WA_CUTS].index(True)
+            n0 = (i - WA_CUTS[u][0]) * P
             a_acc = psum.tile([P, HALF], F32, name="a_acc", tag=f"bank{bank}")
             nc.tensor.matmul_mx(
                 out=a_acc[:],
-                lhsT=wa_w[:, 2 * i * P : 2 * (i + 1) * P].bitcast(FP4X4),
+                lhsT=wa_w[u][:, 2 * n0 : 2 * (n0 + P)].bitcast(FP4X4),
                 lhsT_scale=wa_s[:].bitcast(U8)[:, i * P : (i + 1) * P],
                 rhs=h_q[:, cols].bitcast(FP8X4),
                 rhs_scale=h_s[:, cols],
@@ -202,9 +219,9 @@ def tile_list_session_state_decay_kernel(
             rows = ap.rearrange("p (r c) -> p r c", c=CHUNK)
             nc.gpsimd.tensor_tensor(rows, picked[:, :, :CHUNK].bitcast(F32), rows, ALU.mult)
 
-        def token_product(i, half, bank):
-            cols = slice(half * HALF, (half + 1) * HALF)
-            b_acc = psum.tile([P, HALF], F32, name="b_acc", tag=f"bank{bank}")
+        def token_product(i, j0, width, bank):
+            cols = slice(j0, j0 + width)
+            b_acc = psum.tile([P, width], F32, name="b_acc", tag=f"bank{bank}")
             u = [first <= i < end for first, end in WB_CUTS].index(True)
             n0 = (i - WB_CUTS[u][0]) * P
             for a in range(PASSES):
@@ -229,10 +246,10 @@ def tile_list_session_state_decay_kernel(
         gather_words(0, 0, S)
         cast_w1(0, 64)
         quantize_w1(0)
-        cast_w1(1, 64)
+        cast_w1(1, 44)
         quantize_w1(1)
         for c in range(4):
-            open_chunk(c)
+            open_chunk(c, c)
             hidden_pass(c, 0)
         for q in range(4):
             gather_words(1, q * QUARTER, QUARTER)
@@ -240,52 +257,76 @@ def tile_list_session_state_decay_kernel(
             hidden_pass(c, 1)
             relu(c)
         quantize_h(0)
-        for c in range(4, ROWS):
-            open_chunk(c)
+
+        def hidden_chunk(c, bank):
+            open_chunk(c, bank)
             for a in range(PASSES):
                 hidden_pass(c, a)
             relu(c)
+
+        for c in range(4, ROWS):
+            hidden_chunk(c, c - 4)
         quantize_h(1)
         picked = picked_tile("picked_pair", 2 * ROWS, "picked_pair")[:].rearrange("p (i r) c -> p i r c", i=2)
         for i in range(2):
             gather_state(i, picked[:, i])
-        for i in range(2):
-            rate(i, 0, 4 - 4 * i)
+            rate(i, 0, 4 + i)
         for i in range(2):
             decay(new[i][:, :HALF])
             times_state(new[i][:, :HALF], picked[:, i, : ROWS // 2, :])
+
+        scalar_banks = [6, 7, 5]
+        vector_banks = [0, 1, 4, 2, 3]
+
+        def turn(banks):
+            banks.append(banks.pop(0))
+            return banks[-1]
+
+        def half_of(ap, half):
+            return ap[:, half * HALF : (half + 1) * HALF]
+
+        def add_on_gpsimd(i, j0, b_part):
+            dst = new[i][:, j0 : j0 + b_part.shape[1]]
+            nc.gpsimd.tensor_tensor(dst, b_part, dst, ALU.add)
+            store(i, j0, dst)
+
+        b_pair = keep.tile([P, 2, HALF], F32, name="b_pair")
         for i in range(2):
-            rate(i, 1, 1 + i)
+            nc.scalar.copy(b_pair[:, i, :], token_product(i, 0, HALF, 6 + i)[:])
+        nc.gpsimd.tensor_tensor(new_pair[:, :, :HALF], b_pair[:], new_pair[:, :, :HALF], ALU.add)
+        for i in range(2):
+            store(i, 0, half_of(new[i], 0))
+            rate(i, 1, 4 + i)
         decay(new_pair[:, :, HALF:])
         rows = new_pair[:, :, HALF:].rearrange("p i (r c) -> p i r c", c=CHUNK)
         nc.gpsimd.tensor_tensor(rows, picked[:, :, ROWS // 2 :, :CHUNK].bitcast(F32), rows, ALU.mult)
 
-        b_sb = keep.tile([P, GPSIMD_HALVES * HALF], F32, name="b_sb")
-        for k in range(GPSIMD_HALVES):
-            nc.scalar.copy(b_sb[:, k * HALF : (k + 1) * HALF], token_product(k // 2, k % 2, 5 + k)[:])
-        summed = new_pair[:].rearrange("p i s -> p (i s)")[:, : GPSIMD_HALVES * HALF]
-        nc.gpsimd.tensor_tensor(summed, b_sb[:], summed, ALU.add)
-        store(0, 0, new[0])
-        store(1, 0, new[1][:, :HALF])
         last = TILES - 1
         for i in range(2, TILES):
             picked = picked_tile(f"picked{i}", ROWS, f"picked{i % 4}")
             gather_state(i, picked)
             for half in range(2):
-                rate(i, half, 5 + half if i == 2 else 7 - 2 * half)
+                rate(i, half, 2 + half if i == 3 else turn(scalar_banks))
             if i < last:
                 decay(new[i])
                 times_state(new[i], picked)
             else:
                 for half in range(2):
-                    cols = slice(half * HALF, (half + 1) * HALF)
-                    decay(new[i][:, cols])
-                    times_state(new[i][:, cols], picked[:, half * ROWS // 2 : (half + 1) * ROWS // 2, :])
-            if i == 2:
-                add_on_vector(1, HALF, token_product(1, 1, 6)[:], new[1][:, HALF:])
-        halves = [(i, half) for i in range(2, TILES) for half in range(2)]
-        for k, (i, half) in enumerate(halves[:-1]):
-            add_on_vector(i, half * HALF, token_product(i, half, k % 5)[:], new[i][:, half * HALF : (half + 1) * HALF])
-        b_acc = token_product(last, 1, (len(halves) - 1) % 5)
+                    decay(half_of(new[i], half))
+                    times_state(half_of(new[i], half), picked[:, half * ROWS // 2 : (half + 1) * ROWS // 2, :])
+            if i == 4:
+                b_shared = keep.tile([P, GPSIMD_SHARE], F32, name="b_shared")
+                nc.scalar.copy(b_shared[:], token_product(SHARED_TILE, 0, GPSIMD_SHARE, turn(scalar_banks))[:])
+                add_on_gpsimd(SHARED_TILE, 0, b_shared[:])
+        for i in range(2):
+            add_on_vector(i, HALF, token_product(i, HALF, HALF, 2 + i)[:], half_of(new[i], 1))
+        for i in range(2, last):
+            for half in range(2):
+                j0 = max(half * HALF, GPSIMD_SHARE if i == SHARED_TILE else 0)
+                end = (half + 1) * HALF
+                if end > j0:
+                    add_on_vector(i, j0, token_product(i, j0, end - j0, turn(vector_banks))[:], new[i][:, j0:end])
+        add_on_vector(last, 0, token_product(last, 0, HALF, turn(vector_banks))[:], half_of(new[last], 0))
+        b_last = token_product(last, HALF, HALF, turn(vector_banks))
         for j0 in (HALF, 3 * QUARTER):
-            add_on_vector(last, j0, b_acc[:, j0 - HALF : j0 - HALF + QUARTER], new[last][:, j0 : j0 + QUARTER])
+            add_on_vector(last, j0, b_last[:, j0 - HALF : j0 - HALF + QUARTER], new[last][:, j0 : j0 + QUARTER])

@@ -25,12 +25,14 @@ ROWS = S // CHUNK
 QUARTER = 256
 HALF = 512
 ROW_GAP = 8
-SHARED_TILE = 2
+SHARED_TILE = 6
 GPSIMD_SHARE = 256
 GATHER_ROWS = ((0, 5), (5, 8))
 WA_CUTS = ((0, 2), (2, 8))
 WB_CUTS = ((0, 2), (2, 3), (3, 5), (5, 8))
-WB_BEHIND_STATE = (1, 5, 6, 7)
+WB_BEHIND_STATE = (2, 5, 6, 7)
+V_ROW = (4, 8)
+WB_ROW = 8
 
 
 def tile_list_session_state_decay_kernel(
@@ -87,7 +89,7 @@ def tile_list_session_state_decay_kernel(
 
         def place_scales(a, r):
             rows = v_rows[:].bitcast(I32)[16 * a + r : 16 * a + 16 : 4, :]
-            nc.sync.dma_start(v_s[a][r:P:32, :], rows)
+            nc.sync.dma_start(v_s[a][V_ROW[a] + r : P : 32, :], rows)
 
         def load_state(i):
             nc.sync.dma_start(state[i][:], gT[i * P : (i + 1) * P, :])
@@ -104,33 +106,29 @@ def tile_list_session_state_decay_kernel(
             nc.sync.dma_start(wa_s[r:P:32, :], wa_scales[0, r:16:4, :].bitcast(I32))
 
         def load_wb_scales(r):
-            nc.sync.dma_start(wb_s[r:P:32, :, :], wb_scales[:, r:16:4, :].rearrange("a q n -> q a n").bitcast(I32))
+            nc.sync.dma_start(wb_s[WB_ROW + r : P : 32, :, :], wb_scales[:, r:16:4, :].rearrange("a q n -> q a n").bitcast(I32))
 
         nc.sync.dma_start(offsets[:], offs)
         nc.sync.dma_start(tab_s[:32, :], tab_scales.rearrange("a q t -> (a q) t").bitcast(I32))
-        load_table(0)
         load_w1(0, 0, 4)
+        load_table(0)
         load_w1(1, 0, 4)
         nc.vector.tensor_copy(v_rows[:], tab_s[:].bitcast(U8).indirect(offsets[:]))
-        for r in range(2):
-            load_wa_scales(r)
         for r in range(4):
             place_scales(0, r)
         load_table(1)
-        for r in range(2):
-            load_wb_scales(r)
         for r in range(4):
             place_scales(1, r)
         load_state(0)
         load_state(1)
-        for r in range(2, 4):
+        for r in range(4):
             load_wa_scales(r)
-        load_wb_scales(2)
         load_wa(0)
-        load_wb_scales(3)
-        load_wb(0)
         for i in range(2, TILES):
             load_state(i)
+            if i == 2:
+                for r in range(4):
+                    load_wb_scales(r)
             if i == 3:
                 load_wa(1)
             if i in WB_BEHIND_STATE:
@@ -168,7 +166,7 @@ def tile_list_session_state_decay_kernel(
                     lhsT=w1_q[a][:, r].bitcast(FP8X4),
                     lhsT_scale=w1_s[a][:, r],
                     rhs=v_w[a][:, cols].bitcast(FP8X4),
-                    rhs_scale=v_s[a][:].bitcast(U8)[:, cols],
+                    rhs_scale=v_s[a][V_ROW[a] :, :].bitcast(U8)[:, cols],
                     start=(a == 0 and t == 0),
                     stop=(a == PASSES - 1 and t == PACK - 1),
                 )
@@ -228,9 +226,9 @@ def tile_list_session_state_decay_kernel(
                 nc.tensor.matmul_mx(
                     out=b_acc[:],
                     lhsT=wb_w[u][:, a, n0 : n0 + P].bitcast(FP8X4),
-                    lhsT_scale=wb_s[:, a, :].bitcast(U8)[:, i * P : (i + 1) * P],
+                    lhsT_scale=wb_s[WB_ROW:, a, :].bitcast(U8)[:, i * P : (i + 1) * P],
                     rhs=v_w[a][:, cols].bitcast(FP8X4),
-                    rhs_scale=v_s[a][:].bitcast(U8)[:, cols],
+                    rhs_scale=v_s[a][V_ROW[a] :, :].bitcast(U8)[:, cols],
                     start=(a == 0),
                     stop=(a == PASSES - 1),
                 )
@@ -243,9 +241,9 @@ def tile_list_session_state_decay_kernel(
             nc.vector.tensor_tensor(dst, new[i][:, j0 : j0 + dst.shape[1]], b_acc, ALU.add)
             store(i, j0, dst)
 
-        gather_words(0, 0, S)
-        cast_w1(0, 64)
+        cast_w1(0, 44)
         quantize_w1(0)
+        gather_words(0, 0, S)
         cast_w1(1, 44)
         quantize_w1(1)
         for c in range(4):
@@ -314,19 +312,13 @@ def tile_list_session_state_decay_kernel(
                 for half in range(2):
                     decay(half_of(new[i], half))
                     times_state(half_of(new[i], half), picked[:, half * ROWS // 2 : (half + 1) * ROWS // 2, :])
-            if i == 4:
-                b_shared = keep.tile([P, GPSIMD_SHARE], F32, name="b_shared")
-                nc.scalar.copy(b_shared[:], token_product(SHARED_TILE, 0, GPSIMD_SHARE, turn(scalar_banks))[:])
-                add_on_gpsimd(SHARED_TILE, 0, b_shared[:])
+        b_shared = keep.tile([P, GPSIMD_SHARE], F32, name="b_shared")
+        nc.scalar.copy(b_shared[:], token_product(SHARED_TILE, S - GPSIMD_SHARE, GPSIMD_SHARE, turn(scalar_banks))[:])
         for i in range(2):
             add_on_vector(i, HALF, token_product(i, HALF, HALF, 2 + i)[:], half_of(new[i], 1))
-        for i in range(2, last):
+        for i in range(2, TILES):
             for half in range(2):
-                j0 = max(half * HALF, GPSIMD_SHARE if i == SHARED_TILE else 0)
-                end = (half + 1) * HALF
-                if end > j0:
-                    add_on_vector(i, j0, token_product(i, j0, end - j0, turn(vector_banks))[:], new[i][:, j0:end])
-        add_on_vector(last, 0, token_product(last, 0, HALF, turn(vector_banks))[:], half_of(new[last], 0))
-        b_last = token_product(last, HALF, HALF, turn(vector_banks))
-        for j0 in (HALF, 3 * QUARTER):
-            add_on_vector(last, j0, b_last[:, j0 - HALF : j0 - HALF + QUARTER], new[last][:, j0 : j0 + QUARTER])
+                j0 = half * HALF
+                end = min(j0 + HALF, S - GPSIMD_SHARE if i == SHARED_TILE else S)
+                add_on_vector(i, j0, token_product(i, j0, end - j0, turn(vector_banks))[:], new[i][:, j0:end])
+        add_on_gpsimd(SHARED_TILE, S - GPSIMD_SHARE, b_shared[:])

@@ -28,9 +28,9 @@ ROW_GAP = 8
 SHARED_TILE = 6
 GPSIMD_SHARE = 256
 GATHER_ROWS = ((0, 5), (5, 8))
-WA_CUTS = ((0, 2), (2, 8))
-WB_CUTS = ((0, 2), (2, 3), (3, 5), (5, 8))
-WB_BEHIND_STATE = (2, 5, 6, 7)
+WA_CUTS = ((0, 4), (4, 8))
+WB_CUTS = ((0, 2), (2, 4), (4, 5), (5, 8))
+WB_BEHIND_STATE = (4, 5, 6, 7)
 V_ROW = (4, 8)
 WB_ROW = 8
 
@@ -111,8 +111,8 @@ def tile_list_session_state_decay_kernel(
         nc.sync.dma_start(offsets[:], offs)
         nc.sync.dma_start(tab_s[:32, :], tab_scales.rearrange("a q t -> (a q) t").bitcast(I32))
         load_w1(0, 0, 4)
-        load_table(0)
         load_w1(1, 0, 4)
+        load_table(0)
         nc.vector.tensor_copy(v_rows[:], tab_s[:].bitcast(U8).indirect(offsets[:]))
         for r in range(4):
             place_scales(0, r)
@@ -126,13 +126,13 @@ def tile_list_session_state_decay_kernel(
         load_wa(0)
         for i in range(2, TILES):
             load_state(i)
-            if i == 2:
+            if i == 4:
                 for r in range(4):
                     load_wb_scales(r)
-            if i == 3:
-                load_wa(1)
             if i in WB_BEHIND_STATE:
                 load_wb(WB_BEHIND_STATE.index(i))
+            if i == 4:
+                load_wa(1)
 
         def cast_w1(a, split):
             dst = w1_bf[a][:].rearrange("p (t m j) -> p m t j", t=PACK, j=PACK)
@@ -234,18 +234,15 @@ def tile_list_session_state_decay_kernel(
                 )
             return b_acc
 
-        def store(i, j0, src):
-            nc.sync.dma_start(out[i * P : (i + 1) * P, j0 : j0 + src.shape[1]], src)
-
-        def add_on_vector(i, j0, b_acc, dst):
-            nc.vector.tensor_tensor(dst, new[i][:, j0 : j0 + dst.shape[1]], b_acc, ALU.add)
-            store(i, j0, dst)
+        def store(i, j0, src, queue=nc.sync):
+            queue.dma_start(out[i * P : (i + 1) * P, j0 : j0 + src.shape[1]], src)
 
         cast_w1(0, 44)
         quantize_w1(0)
-        gather_words(0, 0, S)
         cast_w1(1, 44)
         quantize_w1(1)
+        for j0, width in ((0, QUARTER), (QUARTER, QUARTER), (HALF, HALF)):
+            gather_words(0, j0, width)
         for c in range(4):
             open_chunk(c, c)
             hidden_pass(c, 0)
@@ -283,42 +280,54 @@ def tile_list_session_state_decay_kernel(
         def half_of(ap, half):
             return ap[:, half * HALF : (half + 1) * HALF]
 
-        def add_on_gpsimd(i, j0, b_part):
+        def add_on_gpsimd(i, j0, b_part, queue):
             dst = new[i][:, j0 : j0 + b_part.shape[1]]
             nc.gpsimd.tensor_tensor(dst, b_part, dst, ALU.add)
-            store(i, j0, dst)
+            store(i, j0, dst, queue)
 
-        b_pair = keep.tile([P, 2, HALF], F32, name="b_pair")
+        def add_on_vector(i, j0, end, banks=vector_banks):
+            dst = new[i][:, j0:end]
+            nc.vector.tensor_tensor(dst, dst, token_product(i, j0, end - j0, turn(banks))[:], ALU.add)
+
         for i in range(2):
-            nc.scalar.copy(b_pair[:, i, :], token_product(i, 0, HALF, 6 + i)[:])
-        nc.gpsimd.tensor_tensor(new_pair[:, :, :HALF], b_pair[:], new_pair[:, :, :HALF], ALU.add)
+            rate(i, 1, turn(scalar_banks))
         for i in range(2):
-            store(i, 0, half_of(new[i], 0))
-            rate(i, 1, 4 + i)
-        decay(new_pair[:, :, HALF:])
+            decay(half_of(new[i], 1))
         rows = new_pair[:, :, HALF:].rearrange("p i (r c) -> p i r c", c=CHUNK)
         nc.gpsimd.tensor_tensor(rows, picked[:, :, ROWS // 2 :, :CHUNK].bitcast(F32), rows, ALU.mult)
+        for half in range(2):
+            add_on_vector(1, half * HALF, (half + 1) * HALF)
+        store(1, 0, new[1])
 
         last = TILES - 1
         for i in range(2, TILES):
-            picked = picked_tile(f"picked{i}", ROWS, f"picked{i % 4}")
+            picked = picked_tile(f"picked{i}", ROWS, f"picked{i}")
             gather_state(i, picked)
             for half in range(2):
-                rate(i, half, 2 + half if i == 3 else turn(scalar_banks))
+                rate(i, half, turn(scalar_banks))
+            for half in range(2):
+                decay(half_of(new[i], half))
             if i < last:
-                decay(new[i])
                 times_state(new[i], picked)
             else:
                 for half in range(2):
-                    decay(half_of(new[i], half))
                     times_state(half_of(new[i], half), picked[:, half * ROWS // 2 : (half + 1) * ROWS // 2, :])
+            if i == 3:
+                b_first = keep.tile([P, S], F32, name="b_first")
+                for half in range(2):
+                    nc.scalar.copy(half_of(b_first, half), token_product(0, half * HALF, HALF, turn(scalar_banks))[:])
+                add_on_gpsimd(0, 0, b_first[:], nc.sync)
         b_shared = keep.tile([P, GPSIMD_SHARE], F32, name="b_shared")
         nc.scalar.copy(b_shared[:], token_product(SHARED_TILE, S - GPSIMD_SHARE, GPSIMD_SHARE, turn(scalar_banks))[:])
-        for i in range(2):
-            add_on_vector(i, HALF, token_product(i, HALF, HALF, 2 + i)[:], half_of(new[i], 1))
-        for i in range(2, TILES):
-            for half in range(2):
-                j0 = half * HALF
-                end = min(j0 + HALF, S - GPSIMD_SHARE if i == SHARED_TILE else S)
-                add_on_vector(i, j0, token_product(i, j0, end - j0, turn(vector_banks))[:], new[i][:, j0:end])
-        add_on_gpsimd(SHARED_TILE, S - GPSIMD_SHARE, b_shared[:])
+        for i in range(2, last):
+            end = S - GPSIMD_SHARE if i == SHARED_TILE else S
+            add_on_vector(i, 0, HALF)
+            if i > 4:
+                store(i, 0, half_of(new[i], 0))
+            add_on_vector(i, HALF, end)
+            j0 = HALF if i > 4 else 0
+            store(i, j0, new[i][:, j0:end])
+        for half in range(2):
+            add_on_vector(last, half * HALF, (half + 1) * HALF, scalar_banks)
+            store(last, half * HALF, half_of(new[last], half))
+        add_on_gpsimd(SHARED_TILE, S - GPSIMD_SHARE, b_shared[:], nc.scalar)

@@ -20,19 +20,25 @@ P = 128
 PACK = 4
 PASSES = K // (P * PACK)
 TILES = N // P
-CHUNK = 128
-ROWS = S // CHUNK
-QUARTER = 256
-HALF = 512
+LAST = TILES - 1
+CHUNK, QUARTER, HALF = 128, 256, 512
+CHUNKS = S // CHUNK
+SCALE_DMAS = 4
+
+V_FIRST = (4, 8)
+WB_FIRST = 8
+
+SCALAR_CAST = 44
+
 ROW_GAP = 8
-SHARED_TILE = 6
-GPSIMD_SHARE = 256
-GATHER_ROWS = ((0, 5), (5, 8))
-WA_CUTS = ((0, 4), (4, 8))
-WB_CUTS = ((0, 2), (2, 4), (4, 5), (5, 8))
-WB_BEHIND_STATE = (4, 5, 6, 7)
-V_ROW = (4, 8)
-WB_ROW = 8
+GATHER_ROWS = ((0, 5), (5, CHUNKS))
+
+GPSIMD_SHARE = 128
+GPSIMD_SUM_BEHIND = 3
+
+WA_PIECES = ((0, 4), (4, TILES))
+WB_PIECES = ((0, 2), (2, 4), (4, 5), (5, TILES))
+FIRST_WB_BEHIND = 4
 
 
 def tile_list_session_state_decay_kernel(
@@ -49,14 +55,14 @@ def tile_list_session_state_decay_kernel(
         wa_s = keep.tile([P, N // 4], I32, name="wa_s", align_bytes=64)
         wb_s = keep.tile([P, PASSES, N // 4], I32, name="wb_s", align_bytes=64)
         w1_raw = [keep.tile([P, PACK, H], F32, name=f"w1_raw{a}") for a in range(PASSES)]
-        warm = keep.tile([P, 8], F32, name="warm")
         w1_bf = [keep.tile([P, PACK * H], BF16, name=f"w1_bf{a}", align_bytes=64) for a in range(PASSES)]
         w1_s = [keep.tile([P, H], U8, name=f"w1_s{a}", align_bytes=64) for a in range(PASSES)]
         wa_w = [
-            keep.tile([P, 2 * (end - first) * P], U8, name=f"wa_w{first}", align_bytes=64) for first, end in WA_CUTS
+            keep.tile([P, 2 * (end - first) * P], U8, name=f"wa_w{first}", align_bytes=64) for first, end in WA_PIECES
         ]
         wb_w = [
-            keep.tile([P, PASSES, (end - first) * P], I32, name=f"wb_w{first}", align_bytes=64) for first, end in WB_CUTS
+            keep.tile([P, PASSES, (end - first) * P], I32, name=f"wb_w{first}", align_bytes=64)
+            for first, end in WB_PIECES
         ]
         state = [keep.tile([P, T], F32, name=f"state{i}") for i in range(TILES)]
         v_w = [keep.tile([P, S], U32, name=f"v_w{a}", align_bytes=64) for a in range(PASSES)]
@@ -64,86 +70,68 @@ def tile_list_session_state_decay_kernel(
         v_s = [keep.tile([P, S // 4], I32, name=f"v_s{a}", align_bytes=64) for a in range(PASSES)]
         h_q = keep.tile([P, S], U32, name="h_q", align_bytes=64)
         h_s = keep.tile([P, S], U8, name="h_s", align_bytes=64)
-        h_bf = [
-            keep.tile([P, 4, CHUNK * PACK], BF16, name=f"h_bf{u}", tag=f"h_bf{u}", align_bytes=64) for u in range(2)
-        ]
+        h_bf = [keep.tile([P, HALF // CHUNK, CHUNK * PACK], BF16, name=f"h_bf{u}", align_bytes=64) for u in range(2)]
         new_pair = keep.tile([P, 2, S], F32, name="new_pair")
-        new = [new_pair[:, i, :] if i < 2 else keep.tile([P, S], F32, name=f"new{i}", tag=f"new{i}")[:] for i in range(TILES)]
+        new = [new_pair[:, i, :] if i < 2 else keep.tile([P, S], F32, name=f"new{i}")[:] for i in range(TILES)]
 
         nc.vector.memset(tab_s[32:64, :], 0)
         nc.vector.memset(tab_s[64:, :], 0)
         for plane in (v_s[0], v_s[1], wa_s, wb_s):
             nc.vector.memset(plane[:], 0)
 
-        nc.gpsimd.memset(warm[:, :1], 0.0)
-        nc.scalar.activation(warm[:, 4:5], warm[:, :1], ACT.Exp)
-
-        wb_view = wb_words.rearrange("a p n i -> p a (n i)")
-
-        def load_w1(a, first, end):
-            rows = w1[a * P * PACK : (a + 1) * P * PACK, :]
-            nc.sync.dma_start(w1_raw[a][:, first:end, :], rows.rearrange("(p j) c -> p j c", j=PACK)[:, first:end, :])
-
         def load_table(a):
             nc.sync.dma_start(tab_w[a][:], tab_words[a].rearrange("p t i -> p (t i)").bitcast(I32))
 
-        def place_scales(a, r):
-            rows = v_rows[:].bitcast(I32)[16 * a + r : 16 * a + 16 : 4, :]
-            nc.sync.dma_start(v_s[a][V_ROW[a] + r : P : 32, :], rows)
+        def place_scales(a):
+            for r in range(SCALE_DMAS):
+                rows = v_rows[:].bitcast(I32)[16 * a + r : 16 * a + 16 : 4, :]
+                nc.sync.dma_start(v_s[a][V_FIRST[a] + r : P : 32, :], rows)
 
         def load_state(i):
             nc.sync.dma_start(state[i][:], gT[i * P : (i + 1) * P, :])
 
-        def load_wb(u):
-            first, end = WB_CUTS[u]
-            nc.sync.dma_start(wb_w[u][:], wb_view[:, :, first * P * PACK : end * P * PACK].bitcast(I32))
-
         def load_wa(u):
-            first, end = WA_CUTS[u]
+            first, end = WA_PIECES[u]
             nc.sync.dma_start(wa_w[u][:].bitcast(I32), wa_words[0][:, 2 * first * P : 2 * end * P].bitcast(I32))
 
-        def load_wa_scales(r):
-            nc.sync.dma_start(wa_s[r:P:32, :], wa_scales[0, r:16:4, :].bitcast(I32))
-
-        def load_wb_scales(r):
-            nc.sync.dma_start(wb_s[WB_ROW + r : P : 32, :, :], wb_scales[:, r:16:4, :].rearrange("a q n -> q a n").bitcast(I32))
+        def load_wb(u):
+            first, end = WB_PIECES[u]
+            words = wb_words.rearrange("a p n i -> p a (n i)")[:, :, first * P * PACK : end * P * PACK]
+            nc.sync.dma_start(wb_w[u][:], words.bitcast(I32))
 
         nc.sync.dma_start(offsets[:], offs)
         nc.sync.dma_start(tab_s[:32, :], tab_scales.rearrange("a q t -> (a q) t").bitcast(I32))
-        load_w1(0, 0, 4)
-        load_w1(1, 0, 4)
+        for a in range(PASSES):
+            rows = w1[a * P * PACK : (a + 1) * P * PACK, :]
+            nc.sync.dma_start(w1_raw[a][:], rows.rearrange("(p j) c -> p j c", j=PACK))
         load_table(0)
         nc.vector.tensor_copy(v_rows[:], tab_s[:].bitcast(U8).indirect(offsets[:]))
-        for r in range(4):
-            place_scales(0, r)
+        place_scales(0)
         load_table(1)
-        for r in range(4):
-            place_scales(1, r)
+        place_scales(1)
         load_state(0)
         load_state(1)
-        for r in range(4):
-            load_wa_scales(r)
+        for r in range(SCALE_DMAS):
+            nc.sync.dma_start(wa_s[r:P:32, :], wa_scales[0, r:16:4, :].bitcast(I32))
         load_wa(0)
-        for i in range(2, TILES):
+        for i in range(2, FIRST_WB_BEHIND + 1):
             load_state(i)
-            if i == 4:
-                for r in range(4):
-                    load_wb_scales(r)
-            if i in WB_BEHIND_STATE:
-                load_wb(WB_BEHIND_STATE.index(i))
-            if i == 4:
-                load_wa(1)
+        for r in range(SCALE_DMAS):
+            rows = wb_scales[:, r:16:4, :].rearrange("a q n -> q a n")
+            nc.sync.dma_start(wb_s[WB_FIRST + r : P : 32, :, :], rows.bitcast(I32))
+        load_wb(0)
+        load_wa(1)
+        for i in range(FIRST_WB_BEHIND + 1, TILES):
+            load_state(i)
+            load_wb(i - FIRST_WB_BEHIND)
 
-        def cast_w1(a, split):
+        w1_q = []
+        for a in range(PASSES):
             dst = w1_bf[a][:].rearrange("p (t m j) -> p m t j", t=PACK, j=PACK)
             src = w1_raw[a][:].rearrange("p j (m t) -> p m t j", t=PACK)
-            nc.scalar.activation(dst[:, :split], src[:, :split], ACT.Copy)
-            nc.vector.tensor_copy(dst[:, split:], src[:, split:])
-
-        w1_q = {}
-
-        def quantize_w1(a):
-            w1_q[a] = keep.tile([P, H], U32, name=f"w1_q{a}", tag=f"w1_q{a}", align_bytes=64)
+            nc.scalar.activation(dst[:, :SCALAR_CAST], src[:, :SCALAR_CAST], ACT.Copy)
+            nc.vector.tensor_copy(dst[:, SCALAR_CAST:], src[:, SCALAR_CAST:])
+            w1_q.append(keep.tile([P, H], U32, name=f"w1_q{a}", align_bytes=64))
             nc.vector.quantize_mx(out=w1_q[a][:].bitcast(FP8X4), scales=w1_s[a][:], in_=w1_bf[a][:])
 
         def listed(j0, width):
@@ -152,123 +140,113 @@ def tile_list_session_state_decay_kernel(
         def gather_words(a, j0, width):
             nc.vector.tensor_copy(v_w[a][:, j0 : j0 + width], tab_w[a][:].bitcast(U32).indirect(listed(j0, width)))
 
-        h_acc = {}
+        def bank_tile(shape, name, bank):
+            return psum.tile(shape, F32, name=name, tag=f"bank{bank}")
 
-        def open_chunk(c, bank):
-            h_acc[c] = psum.tile([P, PACK, CHUNK], F32, name=f"h_acc{c}", tag=f"bank{bank}")
-
-        def hidden_pass(c, a):
+        def hidden_pass(acc, c, a):
             cols = slice(c * CHUNK, (c + 1) * CHUNK)
             for t in range(PACK):
-                r = slice(t * P, (t + 1) * P)
+                channels = slice(t * P, (t + 1) * P)
                 nc.tensor.matmul_mx(
-                    out=h_acc[c][:, t, :],
-                    lhsT=w1_q[a][:, r].bitcast(FP8X4),
-                    lhsT_scale=w1_s[a][:, r],
+                    out=acc[:, t, :],
+                    lhsT=w1_q[a][:, channels].bitcast(FP8X4),
+                    lhsT_scale=w1_s[a][:, channels],
                     rhs=v_w[a][:, cols].bitcast(FP8X4),
-                    rhs_scale=v_s[a][V_ROW[a] :, :].bitcast(U8)[:, cols],
+                    rhs_scale=v_s[a][V_FIRST[a] :, :].bitcast(U8)[:, cols],
                     start=(a == 0 and t == 0),
                     stop=(a == PASSES - 1 and t == PACK - 1),
                 )
 
-        def relu(c):
-            dst = h_bf[c // 4][:, c % 4, :].rearrange("p (j t) -> p j t", t=PACK)
-            src = h_acc[c][:].rearrange("p t j -> p j t")
-            nc.scalar.activation(dst, src, ACT.Relu)
+        def relu(acc, c):
+            half, place = divmod(c, HALF // CHUNK)
+            dst = h_bf[half][:, place, :].rearrange("p (j t) -> p j t", t=PACK)
+            nc.scalar.activation(dst, acc[:].rearrange("p t j -> p j t"), ACT.Relu)
 
-        def quantize_h(q):
-            cols = slice(q * HALF, (q + 1) * HALF)
+        def quantize_h(half):
+            cols = slice(half * HALF, (half + 1) * HALF)
             nc.vector.quantize_mx(
-                out=h_q[:, cols].bitcast(FP8X4), scales=h_s[:, cols], in_=h_bf[q][:].rearrange("p c w -> p (c w)")
+                out=h_q[:, cols].bitcast(FP8X4), scales=h_s[:, cols], in_=h_bf[half][:].rearrange("p c w -> p (c w)")
             )
 
-        def picked_tile(name, rows, tag):
-            return keep.tile([P, rows, CHUNK + ROW_GAP], U32, name=name, tag=tag, align_bytes=64)
+        for j0, width in ((0, QUARTER), (QUARTER, QUARTER), (HALF, HALF)):
+            gather_words(0, j0, width)
+        opened = []
+        for c in range(CHUNKS // 2):
+            opened.append(bank_tile([P, PACK, CHUNK], f"h_acc{c}", c))
+            hidden_pass(opened[c], c, 0)
+        for j0 in range(0, S, QUARTER):
+            gather_words(1, j0, QUARTER)
+        for c in range(CHUNKS // 2):
+            hidden_pass(opened[c], c, 1)
+            relu(opened[c], c)
+        quantize_h(0)
+        for c in range(CHUNKS // 2, CHUNKS):
+            acc = bank_tile([P, PACK, CHUNK], f"h_acc{c}", c - CHUNKS // 2)
+            for a in range(PASSES):
+                hidden_pass(acc, c, a)
+            relu(acc, c)
+        quantize_h(1)
 
-        def gather_rows(dst, i, first, end):
-            nc.vector.tensor_copy(
-                dst[:, :, :CHUNK], state[i][:].bitcast(U32).indirect(listed(first * CHUNK, (end - first) * CHUNK))
-            )
+        def half_of(ap, half):
+            return ap[:, half * HALF : (half + 1) * HALF]
+
+        def piece_of(pieces, i):
+            u = [first <= i < end for first, end in pieces].index(True)
+            return u, (i - pieces[u][0]) * P
+
+        def picked_tile(name, rows):
+            return keep.tile([P, rows, CHUNK + ROW_GAP], U32, name=name, align_bytes=64)
 
         def gather_state(i, picked):
             for first, end in GATHER_ROWS:
-                gather_rows(picked[:, first:end, :], i, first, end)
+                entries = listed(first * CHUNK, (end - first) * CHUNK)
+                nc.vector.tensor_copy(picked[:, first:end, :CHUNK], state[i][:].bitcast(U32).indirect(entries))
 
         def rate(i, half, bank):
-            cols = slice(half * HALF, (half + 1) * HALF)
-            u = [first <= i < end for first, end in WA_CUTS].index(True)
-            n0 = (i - WA_CUTS[u][0]) * P
-            a_acc = psum.tile([P, HALF], F32, name="a_acc", tag=f"bank{bank}")
+            u, n0 = piece_of(WA_PIECES, i)
+            a_acc = bank_tile([P, HALF], "a_acc", bank)
             nc.tensor.matmul_mx(
                 out=a_acc[:],
                 lhsT=wa_w[u][:, 2 * n0 : 2 * (n0 + P)].bitcast(FP4X4),
                 lhsT_scale=wa_s[:].bitcast(U8)[:, i * P : (i + 1) * P],
-                rhs=h_q[:, cols].bitcast(FP8X4),
-                rhs_scale=h_s[:, cols],
+                rhs=half_of(h_q, half).bitcast(FP8X4),
+                rhs_scale=half_of(h_s, half),
                 start=True,
                 stop=True,
             )
-            nc.scalar.activation(new[i][:, cols], a_acc[:], ACT.Exp)
+            nc.scalar.activation(half_of(new[i], half), a_acc[:], ACT.Exp)
 
-        def decay(ap):
-            nc.scalar.activation(ap, ap, ACT.Exp, scale=-1.0)
+        def decay(i, half):
+            nc.scalar.activation(half_of(new[i], half), half_of(new[i], half), ACT.Exp, scale=-1.0)
 
-        def times_state(ap, picked):
-            rows = ap.rearrange("p (r c) -> p r c", c=CHUNK)
-            nc.gpsimd.tensor_tensor(rows, picked[:, :, :CHUNK].bitcast(F32), rows, ALU.mult)
+        def times_state(decays, picked):
+            nc.gpsimd.tensor_tensor(decays, picked.bitcast(F32), decays, ALU.mult)
+
+        def in_rows(ap):
+            return ap.rearrange("p (r c) -> p r c", c=CHUNK)
 
         def token_product(i, j0, width, bank):
-            cols = slice(j0, j0 + width)
-            b_acc = psum.tile([P, width], F32, name="b_acc", tag=f"bank{bank}")
-            u = [first <= i < end for first, end in WB_CUTS].index(True)
-            n0 = (i - WB_CUTS[u][0]) * P
-            for a in range(PASSES):
-                nc.tensor.matmul_mx(
-                    out=b_acc[:],
-                    lhsT=wb_w[u][:, a, n0 : n0 + P].bitcast(FP8X4),
-                    lhsT_scale=wb_s[WB_ROW:, a, :].bitcast(U8)[:, i * P : (i + 1) * P],
-                    rhs=v_w[a][:, cols].bitcast(FP8X4),
-                    rhs_scale=v_s[a][V_ROW[a] :, :].bitcast(U8)[:, cols],
-                    start=(a == 0),
-                    stop=(a == PASSES - 1),
-                )
+            b_acc = bank_tile([P, width], "b_acc", bank)
+            u, n0 = piece_of(WB_PIECES, i)
+            done = 0
+            for columns in (HALF, QUARTER, CHUNK):
+                if width & columns:
+                    cols = slice(j0 + done, j0 + done + columns)
+                    for a in range(PASSES):
+                        nc.tensor.matmul_mx(
+                            out=b_acc[:, done : done + columns],
+                            lhsT=wb_w[u][:, a, n0 : n0 + P].bitcast(FP8X4),
+                            lhsT_scale=wb_s[WB_FIRST:, a, :].bitcast(U8)[:, i * P : (i + 1) * P],
+                            rhs=v_w[a][:, cols].bitcast(FP8X4),
+                            rhs_scale=v_s[a][V_FIRST[a] :, :].bitcast(U8)[:, cols],
+                            start=(a == 0),
+                            stop=(a == PASSES - 1),
+                        )
+                    done += columns
             return b_acc
 
-        def store(i, j0, src, queue=nc.sync):
-            queue.dma_start(out[i * P : (i + 1) * P, j0 : j0 + src.shape[1]], src)
-
-        cast_w1(0, 44)
-        quantize_w1(0)
-        cast_w1(1, 44)
-        quantize_w1(1)
-        for j0, width in ((0, QUARTER), (QUARTER, QUARTER), (HALF, HALF)):
-            gather_words(0, j0, width)
-        for c in range(4):
-            open_chunk(c, c)
-            hidden_pass(c, 0)
-        for q in range(4):
-            gather_words(1, q * QUARTER, QUARTER)
-        for c in range(4):
-            hidden_pass(c, 1)
-            relu(c)
-        quantize_h(0)
-
-        def hidden_chunk(c, bank):
-            open_chunk(c, bank)
-            for a in range(PASSES):
-                hidden_pass(c, a)
-            relu(c)
-
-        for c in range(4, ROWS):
-            hidden_chunk(c, c - 4)
-        quantize_h(1)
-        picked = picked_tile("picked_pair", 2 * ROWS, "picked_pair")[:].rearrange("p (i r) c -> p i r c", i=2)
-        for i in range(2):
-            gather_state(i, picked[:, i])
-            rate(i, 0, 4 + i)
-        for i in range(2):
-            decay(new[i][:, :HALF])
-            times_state(new[i][:, :HALF], picked[:, i, : ROWS // 2, :])
+        def store(i, j0, end):
+            nc.sync.dma_start(out[i * P : (i + 1) * P, j0:end], new[i][:, j0:end])
 
         scalar_banks = [6, 7, 5]
         vector_banks = [0, 1, 4, 2, 3]
@@ -277,57 +255,59 @@ def tile_list_session_state_decay_kernel(
             banks.append(banks.pop(0))
             return banks[-1]
 
-        def half_of(ap, half):
-            return ap[:, half * HALF : (half + 1) * HALF]
-
-        def add_on_gpsimd(i, j0, b_part, queue):
-            dst = new[i][:, j0 : j0 + b_part.shape[1]]
-            nc.gpsimd.tensor_tensor(dst, b_part, dst, ALU.add)
-            store(i, j0, dst, queue)
-
-        def add_on_vector(i, j0, end, banks=vector_banks):
+        def add_on_vector(i, j0, end, banks):
             dst = new[i][:, j0:end]
             nc.vector.tensor_tensor(dst, dst, token_product(i, j0, end - j0, turn(banks))[:], ALU.add)
 
+        def add_piece(u):
+            for i in range(*WB_PIECES[u]):
+                for half in range(2):
+                    add_on_vector(i, half * HALF, (half + 1) * HALF, vector_banks)
+                store(i, 0, S)
+
+        picked = picked_tile("picked_pair", 2 * CHUNKS)[:].rearrange("p (i r) c -> p i r c", i=2)
+        for i in range(2):
+            gather_state(i, picked[:, i])
+            rate(i, 0, 4 + i)
+        for i in range(2):
+            decay(i, 0)
+            times_state(in_rows(half_of(new[i], 0)), picked[:, i, : CHUNKS // 2, :CHUNK])
         for i in range(2):
             rate(i, 1, turn(scalar_banks))
         for i in range(2):
-            decay(half_of(new[i], 1))
-        rows = new_pair[:, :, HALF:].rearrange("p i (r c) -> p i r c", c=CHUNK)
-        nc.gpsimd.tensor_tensor(rows, picked[:, :, ROWS // 2 :, :CHUNK].bitcast(F32), rows, ALU.mult)
-        for half in range(2):
-            add_on_vector(1, half * HALF, (half + 1) * HALF)
-        store(1, 0, new[1])
+            decay(i, 1)
+        second_halves = new_pair[:, :, HALF:].rearrange("p i (r c) -> p i r c", c=CHUNK)
+        times_state(second_halves, picked[:, :, CHUNKS // 2 :, :CHUNK])
+        add_on_vector(1, GPSIMD_SHARE, HALF, vector_banks)
+        add_on_vector(1, HALF, S, vector_banks)
+        store(1, GPSIMD_SHARE, S)
 
-        last = TILES - 1
         for i in range(2, TILES):
-            picked = picked_tile(f"picked{i}", ROWS, f"picked{i}")
+            picked = picked_tile(f"picked{i}", CHUNKS)
             gather_state(i, picked)
             for half in range(2):
                 rate(i, half, turn(scalar_banks))
             for half in range(2):
-                decay(half_of(new[i], half))
-            if i < last:
-                times_state(new[i], picked)
+                decay(i, half)
+            if i < LAST:
+                times_state(in_rows(new[i]), picked[:, :, :CHUNK])
             else:
                 for half in range(2):
-                    times_state(half_of(new[i], half), picked[:, half * ROWS // 2 : (half + 1) * ROWS // 2, :])
-            if i == 3:
-                b_first = keep.tile([P, S], F32, name="b_first")
+                    rows = slice(half * CHUNKS // 2, (half + 1) * CHUNKS // 2)
+                    times_state(in_rows(half_of(new[i], half)), picked[:, rows, :CHUNK])
+            if i == GPSIMD_SUM_BEHIND:
+                b_copy = keep.tile([P, S + GPSIMD_SHARE], F32, name="b_copy")
                 for half in range(2):
-                    nc.scalar.copy(half_of(b_first, half), token_product(0, half * HALF, HALF, turn(scalar_banks))[:])
-                add_on_gpsimd(0, 0, b_first[:], nc.sync)
-        b_shared = keep.tile([P, GPSIMD_SHARE], F32, name="b_shared")
-        nc.scalar.copy(b_shared[:], token_product(SHARED_TILE, S - GPSIMD_SHARE, GPSIMD_SHARE, turn(scalar_banks))[:])
-        for i in range(2, last):
-            end = S - GPSIMD_SHARE if i == SHARED_TILE else S
-            add_on_vector(i, 0, HALF)
-            if i > 4:
-                store(i, 0, half_of(new[i], 0))
-            add_on_vector(i, HALF, end)
-            j0 = HALF if i > 4 else 0
-            store(i, j0, new[i][:, j0:end])
-        for half in range(2):
-            add_on_vector(last, half * HALF, (half + 1) * HALF, scalar_banks)
-            store(last, half * HALF, half_of(new[last], half))
-        add_on_gpsimd(SHARED_TILE, S - GPSIMD_SHARE, b_shared[:], nc.scalar)
+                    nc.scalar.copy(half_of(b_copy, half), token_product(0, half * HALF, HALF, turn(scalar_banks))[:])
+                nc.scalar.copy(b_copy[:, S:], token_product(1, 0, GPSIMD_SHARE, turn(scalar_banks))[:])
+                dst = new_pair[:].rearrange("p i s -> p (i s)")[:, : S + GPSIMD_SHARE]
+                nc.gpsimd.tensor_tensor(dst, b_copy[:], dst, ALU.add)
+                store(0, 0, S)
+                store(1, 0, GPSIMD_SHARE)
+            if FIRST_WB_BEHIND < i < LAST:
+                add_piece(i - FIRST_WB_BEHIND)
+
+        for i in range(*WB_PIECES[-1]):
+            for half in range(2):
+                add_on_vector(i, half * HALF, (half + 1) * HALF, scalar_banks if i == LAST else vector_banks)
+                store(i, half * HALF, (half + 1) * HALF)

@@ -33,7 +33,7 @@ SCALAR_CAST = 44
 ROW_GAP = 8
 GATHER_ROWS = ((0, 5), (5, CHUNKS))
 
-GPSIMD_SHARE = 128
+GPSIMD_SHARE = 256
 GPSIMD_SUM_BEHIND = 3
 
 WA_PIECES = ((0, 4), (4, TILES))

@@ -33,7 +33,7 @@ SCALAR_CAST = 44
 ROW_GAP = 8
 GATHER_ROWS = ((0, 5), (5, CHUNKS))
 
-GPSIMD_SHARE = 256
+GPSIMD_SHARE = 384
 GPSIMD_SUM_BEHIND = 3
 
 WA_PIECES = ((0, 4), (4, TILES))
@@ -197,10 +197,13 @@ def tile_list_session_state_decay_kernel(
         def picked_tile(name, rows):
             return keep.tile([P, rows, CHUNK + ROW_GAP], U32, name=name, align_bytes=64)
 
+        def gather_rows(i, first, end, rows):
+            entries = listed(first * CHUNK, (end - first) * CHUNK)
+            nc.vector.tensor_copy(rows, state[i][:].bitcast(U32).indirect(entries))
+
         def gather_state(i, picked):
             for first, end in GATHER_ROWS:
-                entries = listed(first * CHUNK, (end - first) * CHUNK)
-                nc.vector.tensor_copy(picked[:, first:end, :CHUNK], state[i][:].bitcast(U32).indirect(entries))
+                gather_rows(i, first, end, picked[:, first:end, :CHUNK])
 
         def rate(i, half, bank):
             u, n0 = piece_of(WA_PIECES, i)
@@ -282,19 +285,14 @@ def tile_list_session_state_decay_kernel(
         add_on_vector(1, HALF, S, vector_banks)
         store(1, GPSIMD_SHARE, S)
 
-        for i in range(2, TILES):
+        for i in range(2, LAST):
             picked = picked_tile(f"picked{i}", CHUNKS)
             gather_state(i, picked)
             for half in range(2):
                 rate(i, half, turn(scalar_banks))
             for half in range(2):
                 decay(i, half)
-            if i < LAST:
-                times_state(in_rows(new[i]), picked[:, :, :CHUNK])
-            else:
-                for half in range(2):
-                    rows = slice(half * CHUNKS // 2, (half + 1) * CHUNKS // 2)
-                    times_state(in_rows(half_of(new[i], half)), picked[:, rows, :CHUNK])
+            times_state(in_rows(new[i]), picked[:, :, :CHUNK])
             if i == GPSIMD_SUM_BEHIND:
                 b_copy = keep.tile([P, S + GPSIMD_SHARE], F32, name="b_copy")
                 for half in range(2):
@@ -304,10 +302,35 @@ def tile_list_session_state_decay_kernel(
                 nc.gpsimd.tensor_tensor(dst, b_copy[:], dst, ALU.add)
                 store(0, 0, S)
                 store(1, 0, GPSIMD_SHARE)
-            if FIRST_WB_BEHIND < i < LAST:
+            if i > FIRST_WB_BEHIND:
                 add_piece(i - FIRST_WB_BEHIND)
 
-        for i in range(*WB_PIECES[-1]):
-            for half in range(2):
-                add_on_vector(i, half * HALF, (half + 1) * HALF, scalar_banks if i == LAST else vector_banks)
-                store(i, half * HALF, (half + 1) * HALF)
+        cut = GATHER_ROWS[0][1]
+        between = WB_PIECES[-1][0]
+        early = picked_tile("picked_last", cut)[:, :, :CHUNK]
+        gather_rows(LAST, 0, cut, early)
+        first_half = keep.tile([P, HALF], F32, name="first_half")
+        b_acc = token_product(between, 0, HALF, turn(vector_banks))
+        nc.vector.tensor_tensor(first_half[:], half_of(new[between], 0), b_acc[:], ALU.add)
+        nc.sync.dma_start(out[between * P : (between + 1) * P, :HALF], first_half[:])
+        add_on_vector(between, HALF, S, vector_banks)
+        store(between, HALF, S)
+        pitch = CHUNK + ROW_GAP
+        late = new[between].bitcast(U32)[:, : (CHUNKS - cut) * pitch].rearrange("p (r c) -> p r c", c=pitch)
+        late = late[:, :, :CHUNK]
+        gather_rows(LAST, cut, CHUNKS, late)
+        for half in range(2):
+            rate(LAST, half, turn(scalar_banks))
+        for half in range(2):
+            decay(LAST, half)
+        times_state(in_rows(new[LAST][:, : cut * CHUNK]), early)
+        times_state(in_rows(new[LAST][:, cut * CHUNK :]), late)
+
+        for half in range(2):
+            add_on_vector(LAST - 1, half * HALF, (half + 1) * HALF, vector_banks)
+            store(LAST - 1, half * HALF, (half + 1) * HALF)
+        add_on_vector(LAST, 0, HALF, scalar_banks)
+        add_on_vector(LAST, HALF, cut * CHUNK, scalar_banks)
+        store(LAST, 0, cut * CHUNK)
+        add_on_vector(LAST, cut * CHUNK, S, scalar_banks)
+        store(LAST, cut * CHUNK, S)

@@ -30,7 +30,7 @@ WB_FIRST = 8
 
 SCALAR_CAST = 44
 
-ROW_GAP = 8
+ROW_GAP = 0
 GATHER_ROWS = ((0, 5), (5, CHUNKS))
 
 GPSIMD_SHARE = 384
@@ -110,11 +110,10 @@ def tile_list_session_state_decay_kernel(
         load_table(1)
         place_scales(1)
         load_state(0)
-        load_state(1)
         for r in range(SCALE_DMAS):
             nc.sync.dma_start(wa_s[r:P:32, :], wa_scales[0, r:16:4, :].bitcast(I32))
         load_wa(0)
-        for i in range(2, FIRST_WB_BEHIND + 1):
+        for i in range(1, FIRST_WB_BEHIND + 1):
             load_state(i)
         for r in range(SCALE_DMAS):
             rows = wb_scales[:, r:16:4, :].rearrange("a q n -> q a n")
@@ -287,7 +286,7 @@ def tile_list_session_state_decay_kernel(
 
         for i in range(2, LAST):
             picked = picked_tile(f"picked{i}", CHUNKS)
-            gather_state(i, picked)
+            gather_rows(i, 0, CHUNKS, picked[:])
             for half in range(2):
                 rate(i, half, turn(scalar_banks))
             for half in range(2):

@@ -29,6 +29,7 @@ V_FIRST = (4, 8)
 WB_FIRST = 8
 
 SCALAR_CAST = 44
+WARM_UPS = 5
 
 ROW_GAP = 0
 GATHER_ROWS = ((0, 5), (5, CHUNKS))
@@ -55,7 +56,6 @@ def tile_list_session_state_decay_kernel(
         wa_s = keep.tile([P, N // 4], I32, name="wa_s", align_bytes=64)
         wb_s = keep.tile([P, PASSES, N // 4], I32, name="wb_s", align_bytes=64)
         w1_raw = [keep.tile([P, PACK, H], F32, name=f"w1_raw{a}") for a in range(PASSES)]
-        w1_bf = [keep.tile([P, PACK * H], BF16, name=f"w1_bf{a}", align_bytes=64) for a in range(PASSES)]
         w1_s = [keep.tile([P, H], U8, name=f"w1_s{a}", align_bytes=64) for a in range(PASSES)]
         wa_w = [
             keep.tile([P, 2 * (end - first) * P], U8, name=f"wa_w{first}", align_bytes=64) for first, end in WA_PIECES
@@ -126,12 +126,13 @@ def tile_list_session_state_decay_kernel(
 
         w1_q = []
         for a in range(PASSES):
-            dst = w1_bf[a][:].rearrange("p (t m j) -> p m t j", t=PACK, j=PACK)
+            w1_bf = keep.tile([P, PACK * H], BF16, name="w1_bf", align_bytes=64)
+            dst = w1_bf[:].rearrange("p (t m j) -> p m t j", t=PACK, j=PACK)
             src = w1_raw[a][:].rearrange("p j (m t) -> p m t j", t=PACK)
             nc.scalar.activation(dst[:, :SCALAR_CAST], src[:, :SCALAR_CAST], ACT.Copy)
             nc.vector.tensor_copy(dst[:, SCALAR_CAST:], src[:, SCALAR_CAST:])
             w1_q.append(keep.tile([P, H], U32, name=f"w1_q{a}", align_bytes=64))
-            nc.vector.quantize_mx(out=w1_q[a][:].bitcast(FP8X4), scales=w1_s[a][:], in_=w1_bf[a][:])
+            nc.vector.quantize_mx(out=w1_q[a][:].bitcast(FP8X4), scales=w1_s[a][:], in_=w1_bf[:])
 
         def listed(j0, width):
             return offsets[:, j0 // 16 : (j0 + width) // 16]
@@ -165,6 +166,18 @@ def tile_list_session_state_decay_kernel(
             cols = slice(half * HALF, (half + 1) * HALF)
             nc.vector.quantize_mx(
                 out=h_q[:, cols].bitcast(FP8X4), scales=h_s[:, cols], in_=h_bf[half][:].rearrange("p c w -> p (c w)")
+            )
+
+        unread = bank_tile([P, HALF], "unread", 7)
+        for step in range(WARM_UPS):
+            nc.tensor.matmul_mx(
+                out=unread[:],
+                lhsT=w1_q[0][:, :P].bitcast(FP8X4),
+                lhsT_scale=w1_s[0][:, :P],
+                rhs=w1_q[0][:].bitcast(FP8X4),
+                rhs_scale=w1_s[0][:],
+                start=True,
+                stop=True,
             )
 
         for j0, width in ((0, QUARTER), (QUARTER, QUARTER), (HALF, HALF)):

@@ -29,12 +29,12 @@ V_FIRST = (4, 8)
 WB_FIRST = 8
 
 SCALAR_CAST = 44
+
 WARM_UPS = 5
 
-ROW_GAP = 0
-GATHER_ROWS = ((0, 5), (5, CHUNKS))
+CUT = 5 * CHUNK
 
-GPSIMD_SHARE = 384
+GPSIMD_SHARE = HALF
 GPSIMD_SUM_BEHIND = 3
 
 WA_PIECES = ((0, 4), (4, TILES))
@@ -169,7 +169,7 @@ def tile_list_session_state_decay_kernel(
             )
 
         unread = bank_tile([P, HALF], "unread", 7)
-        for step in range(WARM_UPS):
+        for warm_up in range(WARM_UPS):
             nc.tensor.matmul_mx(
                 out=unread[:],
                 lhsT=w1_q[0][:, :P].bitcast(FP8X4),
@@ -206,16 +206,11 @@ def tile_list_session_state_decay_kernel(
             u = [first <= i < end for first, end in pieces].index(True)
             return u, (i - pieces[u][0]) * P
 
-        def picked_tile(name, rows):
-            return keep.tile([P, rows, CHUNK + ROW_GAP], U32, name=name, align_bytes=64)
+        def picked_tile(name, shape):
+            return keep.tile(shape, U32, name=name, align_bytes=64)
 
-        def gather_rows(i, first, end, rows):
-            entries = listed(first * CHUNK, (end - first) * CHUNK)
-            nc.vector.tensor_copy(rows, state[i][:].bitcast(U32).indirect(entries))
-
-        def gather_state(i, picked):
-            for first, end in GATHER_ROWS:
-                gather_rows(i, first, end, picked[:, first:end, :CHUNK])
+        def gather_state(i, j0, end, picked):
+            nc.vector.tensor_copy(picked, state[i][:].bitcast(U32).indirect(listed(j0, end - j0)))
 
         def rate(i, half, bank):
             u, n0 = piece_of(WA_PIECES, i)
@@ -236,9 +231,6 @@ def tile_list_session_state_decay_kernel(
 
         def times_state(decays, picked):
             nc.gpsimd.tensor_tensor(decays, picked.bitcast(F32), decays, ALU.mult)
-
-        def in_rows(ap):
-            return ap.rearrange("p (r c) -> p r c", c=CHUNK)
 
         def token_product(i, j0, width, bank):
             b_acc = bank_tile([P, width], "b_acc", bank)
@@ -280,31 +272,30 @@ def tile_list_session_state_decay_kernel(
                     add_on_vector(i, half * HALF, (half + 1) * HALF, vector_banks)
                 store(i, 0, S)
 
-        picked = picked_tile("picked_pair", 2 * CHUNKS)[:].rearrange("p (i r) c -> p i r c", i=2)
+        picked_pair = picked_tile("picked_pair", [P, 2, S])
         for i in range(2):
-            gather_state(i, picked[:, i])
+            for j0, end in ((0, CUT), (CUT, S)):
+                gather_state(i, j0, end, picked_pair[:, i, j0:end])
             rate(i, 0, 4 + i)
         for i in range(2):
             decay(i, 0)
-            times_state(in_rows(half_of(new[i], 0)), picked[:, i, : CHUNKS // 2, :CHUNK])
+            times_state(half_of(new[i], 0), picked_pair[:, i, :HALF])
         for i in range(2):
             rate(i, 1, turn(scalar_banks))
         for i in range(2):
             decay(i, 1)
-        second_halves = new_pair[:, :, HALF:].rearrange("p i (r c) -> p i r c", c=CHUNK)
-        times_state(second_halves, picked[:, :, CHUNKS // 2 :, :CHUNK])
-        add_on_vector(1, GPSIMD_SHARE, HALF, vector_banks)
-        add_on_vector(1, HALF, S, vector_banks)
+        times_state(new_pair[:, :, HALF:], picked_pair[:, :, HALF:])
+        add_on_vector(1, GPSIMD_SHARE, S, vector_banks)
         store(1, GPSIMD_SHARE, S)
 
         for i in range(2, LAST):
-            picked = picked_tile(f"picked{i}", CHUNKS)
-            gather_rows(i, 0, CHUNKS, picked[:])
+            picked = picked_tile(f"picked{i}", [P, S])
+            gather_state(i, 0, S, picked[:])
             for half in range(2):
                 rate(i, half, turn(scalar_banks))
             for half in range(2):
                 decay(i, half)
-            times_state(in_rows(new[i]), picked[:, :, :CHUNK])
+            times_state(new[i], picked[:])
             if i == GPSIMD_SUM_BEHIND:
                 b_copy = keep.tile([P, S + GPSIMD_SHARE], F32, name="b_copy")
                 for half in range(2):
@@ -317,32 +308,29 @@ def tile_list_session_state_decay_kernel(
             if i > FIRST_WB_BEHIND:
                 add_piece(i - FIRST_WB_BEHIND)
 
-        cut = GATHER_ROWS[0][1]
         between = WB_PIECES[-1][0]
-        early = picked_tile("picked_last", cut)[:, :, :CHUNK]
-        gather_rows(LAST, 0, cut, early)
+        early = picked_tile("picked_early", [P, CUT])
+        gather_state(LAST, 0, CUT, early[:])
         first_half = keep.tile([P, HALF], F32, name="first_half")
         b_acc = token_product(between, 0, HALF, turn(vector_banks))
         nc.vector.tensor_tensor(first_half[:], half_of(new[between], 0), b_acc[:], ALU.add)
         nc.sync.dma_start(out[between * P : (between + 1) * P, :HALF], first_half[:])
         add_on_vector(between, HALF, S, vector_banks)
         store(between, HALF, S)
-        pitch = CHUNK + ROW_GAP
-        late = new[between].bitcast(U32)[:, : (CHUNKS - cut) * pitch].rearrange("p (r c) -> p r c", c=pitch)
-        late = late[:, :, :CHUNK]
-        gather_rows(LAST, cut, CHUNKS, late)
+        late = new[between].bitcast(U32)[:, : S - CUT]
+        gather_state(LAST, CUT, S, late)
         for half in range(2):
             rate(LAST, half, turn(scalar_banks))
         for half in range(2):
             decay(LAST, half)
-        times_state(in_rows(new[LAST][:, : cut * CHUNK]), early)
-        times_state(in_rows(new[LAST][:, cut * CHUNK :]), late)
+        times_state(new[LAST][:, :CUT], early[:])
+        times_state(new[LAST][:, CUT:], late)
 
         for half in range(2):
             add_on_vector(LAST - 1, half * HALF, (half + 1) * HALF, vector_banks)
             store(LAST - 1, half * HALF, (half + 1) * HALF)
         add_on_vector(LAST, 0, HALF, scalar_banks)
-        add_on_vector(LAST, HALF, cut * CHUNK, scalar_banks)
-        store(LAST, 0, cut * CHUNK)
-        add_on_vector(LAST, cut * CHUNK, S, scalar_banks)
-        store(LAST, cut * CHUNK, S)
+        add_on_vector(LAST, HALF, CUT, scalar_banks)
+        store(LAST, 0, CUT)
+        add_on_vector(LAST, CUT, S, scalar_banks)
+        store(LAST, CUT, S)

@@ -23,6 +23,7 @@ TILES = N // P
 LAST = TILES - 1
 CHUNK, QUARTER, HALF = 128, 256, 512
 CHUNKS = S // CHUNK
+ALIGN = 256
 SCALE_DMAS = 4
 
 V_FIRST = (4, 8)
@@ -51,28 +52,29 @@ def tile_list_session_state_decay_kernel(
         psum = ctx.enter_context(tc.psum_pool(name="psum", bufs=1))
 
         offsets = keep.tile([P, S // 16], U16, name="offsets")
-        tab_w = [keep.tile([P, T], I32, name=f"tab_w{a}", align_bytes=64) for a in range(PASSES)]
-        tab_s = keep.tile([P, T // 4], I32, name="tab_s", align_bytes=64)
-        wa_s = keep.tile([P, N // 4], I32, name="wa_s", align_bytes=64)
-        wb_s = keep.tile([P, PASSES, N // 4], I32, name="wb_s", align_bytes=64)
-        w1_raw = [keep.tile([P, PACK, H], F32, name=f"w1_raw{a}") for a in range(PASSES)]
-        w1_s = [keep.tile([P, H], U8, name=f"w1_s{a}", align_bytes=64) for a in range(PASSES)]
+        tab_w = [keep.tile([P, T], I32, name=f"tab_w{a}", align_bytes=ALIGN) for a in range(PASSES)]
+        tab_s = keep.tile([P, T // 4], I32, name="tab_s", align_bytes=ALIGN)
+        wa_s = keep.tile([P, N // 4], I32, name="wa_s", align_bytes=ALIGN)
+        wb_s = keep.tile([P, PASSES, N // 4], I32, name="wb_s", align_bytes=ALIGN)
+        w1_raw = [keep.tile([P, PACK, H], F32, name=f"w1_raw{a}", align_bytes=ALIGN) for a in range(PASSES)]
+        w1_s = [keep.tile([P, H], U8, name=f"w1_s{a}", align_bytes=ALIGN) for a in range(PASSES)]
         wa_w = [
-            keep.tile([P, 2 * (end - first) * P], U8, name=f"wa_w{first}", align_bytes=64) for first, end in WA_PIECES
+            keep.tile([P, 2 * (end - first) * P], U8, name=f"wa_w{first}", align_bytes=ALIGN) for first, end in WA_PIECES
         ]
         wb_w = [
-            keep.tile([P, PASSES, (end - first) * P], I32, name=f"wb_w{first}", align_bytes=64)
+            keep.tile([P, PASSES, (end - first) * P], I32, name=f"wb_w{first}", align_bytes=ALIGN)
             for first, end in WB_PIECES
         ]
-        state = [keep.tile([P, T], F32, name=f"state{i}") for i in range(TILES)]
-        v_w = [keep.tile([P, S], U32, name=f"v_w{a}", align_bytes=64) for a in range(PASSES)]
-        v_rows = keep.tile([P, S], U8, name="v_rows", align_bytes=64)
-        v_s = [keep.tile([P, S // 4], I32, name=f"v_s{a}", align_bytes=64) for a in range(PASSES)]
-        h_q = keep.tile([P, S], U32, name="h_q", align_bytes=64)
-        h_s = keep.tile([P, S], U8, name="h_s", align_bytes=64)
-        h_bf = [keep.tile([P, HALF // CHUNK, CHUNK * PACK], BF16, name=f"h_bf{u}", align_bytes=64) for u in range(2)]
-        new_pair = keep.tile([P, 2, S], F32, name="new_pair")
-        new = [new_pair[:, i, :] if i < 2 else keep.tile([P, S], F32, name=f"new{i}")[:] for i in range(TILES)]
+        state = [keep.tile([P, T], F32, name=f"state{i}", align_bytes=ALIGN) for i in range(TILES)]
+        v_w = [keep.tile([P, S], U32, name=f"v_w{a}", align_bytes=ALIGN) for a in range(PASSES)]
+        v_rows = keep.tile([P, S], U8, name="v_rows", align_bytes=ALIGN)
+        v_s = [keep.tile([P, S // 4], I32, name=f"v_s{a}", align_bytes=ALIGN) for a in range(PASSES)]
+        h_q = keep.tile([P, S], U32, name="h_q", align_bytes=ALIGN)
+        h_s = keep.tile([P, S], U8, name="h_s", align_bytes=ALIGN)
+        h_bf = [keep.tile([P, HALF // CHUNK, CHUNK * PACK], BF16, name=f"h_bf{u}", align_bytes=ALIGN) for u in range(2)]
+        new_pair = keep.tile([P, 2, S], F32, name="new_pair", align_bytes=ALIGN)
+        new = [new_pair[:, i, :] for i in range(2)]
+        new.extend(keep.tile([P, S], F32, name=f"new{i}", align_bytes=ALIGN)[:] for i in range(2, TILES))
 
         nc.vector.memset(tab_s[32:64, :], 0)
         nc.vector.memset(tab_s[64:, :], 0)
@@ -126,12 +128,12 @@ def tile_list_session_state_decay_kernel(
 
         w1_q = []
         for a in range(PASSES):
-            w1_bf = keep.tile([P, PACK * H], BF16, name="w1_bf", align_bytes=64)
+            w1_bf = keep.tile([P, PACK * H], BF16, name="w1_bf", align_bytes=ALIGN)
             dst = w1_bf[:].rearrange("p (t m j) -> p m t j", t=PACK, j=PACK)
             src = w1_raw[a][:].rearrange("p j (m t) -> p m t j", t=PACK)
             nc.scalar.activation(dst[:, :SCALAR_CAST], src[:, :SCALAR_CAST], ACT.Copy)
             nc.vector.tensor_copy(dst[:, SCALAR_CAST:], src[:, SCALAR_CAST:])
-            w1_q.append(keep.tile([P, H], U32, name=f"w1_q{a}", align_bytes=64))
+            w1_q.append(keep.tile([P, H], U32, name=f"w1_q{a}", align_bytes=ALIGN))
             nc.vector.quantize_mx(out=w1_q[a][:].bitcast(FP8X4), scales=w1_s[a][:], in_=w1_bf[:])
 
         def listed(j0, width):
@@ -207,7 +209,7 @@ def tile_list_session_state_decay_kernel(
             return u, (i - pieces[u][0]) * P
 
         def picked_tile(name, shape):
-            return keep.tile(shape, U32, name=name, align_bytes=64)
+            return keep.tile(shape, U32, name=name, align_bytes=ALIGN)
 
         def gather_state(i, j0, end, picked):
             nc.vector.tensor_copy(picked, state[i][:].bitcast(U32).indirect(listed(j0, end - j0)))
@@ -311,7 +313,7 @@ def tile_list_session_state_decay_kernel(
         between = WB_PIECES[-1][0]
         early = picked_tile("picked_early", [P, CUT])
         gather_state(LAST, 0, CUT, early[:])
-        first_half = keep.tile([P, HALF], F32, name="first_half")
+        first_half = keep.tile([P, HALF], F32, name="first_half", align_bytes=ALIGN)
         b_acc = token_product(between, 0, HALF, turn(vector_banks))
         nc.vector.tensor_tensor(first_half[:], half_of(new[between], 0), b_acc[:], ALU.add)
         nc.sync.dma_start(out[between * P : (between + 1) * P, :HALF], first_half[:])

from contextlib import ExitStack

import concourse.mybir as mybir

K, T, S, H, N = 1024, 2048, 1024, 512, 1024
FLOPS = 2 * S * (K * H + H * N + K * N)

F32 = mybir.dt.float32
BF16 = mybir.dt.bfloat16
I32 = mybir.dt.int32
U32 = mybir.dt.uint32
U16 = mybir.dt.uint16
U8 = mybir.dt.uint8
FP8X4 = mybir.dt.float8_e4m3fn_x4
FP4X4 = mybir.dt.float4_e2m1fn_x4
ACT = mybir.ActivationFunctionType
ALU = mybir.AluOpType

P = 128
PACK = 4
PASSES = K // (P * PACK)
TILES = N // P
LAST = TILES - 1
CHUNK, QUARTER, HALF = 128, 256, 512
CHUNKS = S // CHUNK
ALIGN = 256
SCALE_DMAS = 4

V_FIRST = (4, 8)
WB_FIRST = 8

SCALAR_CAST = 44

WARM_UPS = 5

CUT = 5 * CHUNK

GPSIMD_SHARE = HALF
GPSIMD_SUM_BEHIND = 3

WA_PIECES = ((0, 4), (4, TILES))
WB_PIECES = ((0, 2), (2, 4), (4, 5), (5, TILES))
FIRST_WB_BEHIND = 4


def tile_list_session_state_decay_kernel(
    tc, tab_words, tab_scales, offs, w1, wa_words, wa_scales, wb_words, wb_scales, gT, out
):
    nc = tc.nc
    with ExitStack() as ctx:
        keep = ctx.enter_context(tc.tile_pool(name="keep", bufs=1))
        psum = ctx.enter_context(tc.psum_pool(name="psum", bufs=1))

        offsets = keep.tile([P, S // 16], U16, name="offsets")
        tab_w = [keep.tile([P, T], I32, name=f"tab_w{a}", align_bytes=ALIGN) for a in range(PASSES)]
        tab_s = keep.tile([P, T // 4], I32, name="tab_s", align_bytes=ALIGN)
        wa_s = keep.tile([P, N // 4], I32, name="wa_s", align_bytes=ALIGN)
        wb_s = keep.tile([P, PASSES, N // 4], I32, name="wb_s", align_bytes=ALIGN)
        w1_raw = [keep.tile([P, PACK, H], F32, name=f"w1_raw{a}", align_bytes=ALIGN) for a in range(PASSES)]
        w1_s = [keep.tile([P, H], U8, name=f"w1_s{a}", align_bytes=ALIGN) for a in range(PASSES)]
        wa_w = [
            keep.tile([P, 2 * (end - first) * P], U8, name=f"wa_w{first}", align_bytes=ALIGN) for first, end in WA_PIECES
        ]
        wb_w = [
            keep.tile([P, PASSES, (end - first) * P], I32, name=f"wb_w{first}", align_bytes=ALIGN)
            for first, end in WB_PIECES
        ]
        state = [keep.tile([P, T], F32, name=f"state{i}", align_bytes=ALIGN) for i in range(TILES)]
        v_w = [keep.tile([P, S], U32, name=f"v_w{a}", align_bytes=ALIGN) for a in range(PASSES)]
        v_rows = keep.tile([P, S], U8, name="v_rows", align_bytes=ALIGN)
        v_s = [keep.tile([P, S // 4], I32, name=f"v_s{a}", align_bytes=ALIGN) for a in range(PASSES)]
        h_q = keep.tile([P, S], U32, name="h_q", align_bytes=ALIGN)
        h_s = keep.tile([P, S], U8, name="h_s", align_bytes=ALIGN)
        h_bf = [keep.tile([P, HALF // CHUNK, CHUNK * PACK], BF16, name=f"h_bf{u}", align_bytes=ALIGN) for u in range(2)]
        new_pair = keep.tile([P, 2, S], F32, name="new_pair", align_bytes=ALIGN)
        new = [new_pair[:, i, :] for i in range(2)]
        new.extend(keep.tile([P, S], F32, name=f"new{i}", align_bytes=ALIGN)[:] for i in range(2, TILES))

        nc.vector.memset(tab_s[32:64, :], 0)
        nc.vector.memset(tab_s[64:, :], 0)
        for plane in (v_s[0], v_s[1], wa_s, wb_s):
            nc.vector.memset(plane[:], 0)

        def load_table(a):
            nc.sync.dma_start(tab_w[a][:], tab_words[a].rearrange("p t i -> p (t i)").bitcast(I32))

        def place_scales(a):
            for r in range(SCALE_DMAS):
                rows = v_rows[:].bitcast(I32)[16 * a + r : 16 * a + 16 : 4, :]
                nc.sync.dma_start(v_s[a][V_FIRST[a] + r : P : 32, :], rows)

        def load_state(i):
            nc.sync.dma_start(state[i][:], gT[i * P : (i + 1) * P, :])

        def load_wa(u):
            first, end = WA_PIECES[u]
            nc.sync.dma_start(wa_w[u][:].bitcast(I32), wa_words[0][:, 2 * first * P : 2 * end * P].bitcast(I32))

        def load_wb(u):
            first, end = WB_PIECES[u]
            words = wb_words.rearrange("a p n i -> p a (n i)")[:, :, first * P * PACK : end * P * PACK]
            nc.sync.dma_start(wb_w[u][:], words.bitcast(I32))

        nc.sync.dma_start(offsets[:], offs)
        nc.sync.dma_start(tab_s[:32, :], tab_scales.rearrange("a q t -> (a q) t").bitcast(I32))
        for a in range(PASSES):
            rows = w1[a * P * PACK : (a + 1) * P * PACK, :]
            nc.sync.dma_start(w1_raw[a][:], rows.rearrange("(p j) c -> p j c", j=PACK))
        load_table(0)
        nc.vector.tensor_copy(v_rows[:], tab_s[:].bitcast(U8).indirect(offsets[:]))
        place_scales(0)
        load_table(1)
        place_scales(1)
        load_state(0)
        for r in range(SCALE_DMAS):
            nc.sync.dma_start(wa_s[r:P:32, :], wa_scales[0, r:16:4, :].bitcast(I32))
        load_wa(0)
        for i in range(1, FIRST_WB_BEHIND + 1):
            load_state(i)
        for r in range(SCALE_DMAS):
            rows = wb_scales[:, r:16:4, :].rearrange("a q n -> q a n")
            nc.sync.dma_start(wb_s[WB_FIRST + r : P : 32, :, :], rows.bitcast(I32))
        load_wb(0)
        load_wa(1)
        for i in range(FIRST_WB_BEHIND + 1, TILES):
            load_state(i)
            load_wb(i - FIRST_WB_BEHIND)

        w1_q = []
        for a in range(PASSES):
            w1_bf = keep.tile([P, PACK * H], BF16, name="w1_bf", align_bytes=ALIGN)
            dst = w1_bf[:].rearrange("p (t m j) -> p m t j", t=PACK, j=PACK)
            src = w1_raw[a][:].rearrange("p j (m t) -> p m t j", t=PACK)
            nc.scalar.activation(dst[:, :SCALAR_CAST], src[:, :SCALAR_CAST], ACT.Copy)
            nc.vector.tensor_copy(dst[:, SCALAR_CAST:], src[:, SCALAR_CAST:])
            w1_q.append(keep.tile([P, H], U32, name=f"w1_q{a}", align_bytes=ALIGN))
            nc.vector.quantize_mx(out=w1_q[a][:].bitcast(FP8X4), scales=w1_s[a][:], in_=w1_bf[:])

        def listed(j0, width):
            return offsets[:, j0 // 16 : (j0 + width) // 16]

        def gather_words(a, j0, width):
            nc.vector.tensor_copy(v_w[a][:, j0 : j0 + width], tab_w[a][:].bitcast(U32).indirect(listed(j0, width)))

        def bank_tile(shape, name, bank):
            return psum.tile(shape, F32, name=name, tag=f"bank{bank}")

        def hidden_pass(acc, c, a):
            cols = slice(c * CHUNK, (c + 1) * CHUNK)
            for t in range(PACK):
                channels = slice(t * P, (t + 1) * P)
                nc.tensor.matmul_mx(
                    out=acc[:, t, :],
                    lhsT=w1_q[a][:, channels].bitcast(FP8X4),
                    lhsT_scale=w1_s[a][:, channels],
                    rhs=v_w[a][:, cols].bitcast(FP8X4),
                    rhs_scale=v_s[a][V_FIRST[a] :, :].bitcast(U8)[:, cols],
                    start=(a == 0 and t == 0),
                    stop=(a == PASSES - 1 and t == PACK - 1),
                )

        def relu(acc, c):
            half, place = divmod(c, HALF // CHUNK)
            dst = h_bf[half][:, place, :].rearrange("p (j t) -> p j t", t=PACK)
            nc.scalar.activation(dst, acc[:].rearrange("p t j -> p j t"), ACT.Relu)

        def quantize_h(half):
            cols = slice(half * HALF, (half + 1) * HALF)
            nc.vector.quantize_mx(
                out=h_q[:, cols].bitcast(FP8X4), scales=h_s[:, cols], in_=h_bf[half][:].rearrange("p c w -> p (c w)")
            )

        unread = bank_tile([P, HALF], "unread", 7)
        for warm_up in range(WARM_UPS):
            nc.tensor.matmul_mx(
                out=unread[:],
                lhsT=w1_q[0][:, :P].bitcast(FP8X4),
                lhsT_scale=w1_s[0][:, :P],
                rhs=w1_q[0][:].bitcast(FP8X4),
                rhs_scale=w1_s[0][:],
                start=True,
                stop=True,
            )

        for j0, width in ((0, QUARTER), (QUARTER, QUARTER), (HALF, HALF)):
            gather_words(0, j0, width)
        opened = []
        for c in range(CHUNKS // 2):
            opened.append(bank_tile([P, PACK, CHUNK], f"h_acc{c}", c))
            hidden_pass(opened[c], c, 0)
        for j0 in range(0, S, QUARTER):
            gather_words(1, j0, QUARTER)
        for c in range(CHUNKS // 2):
            hidden_pass(opened[c], c, 1)
            relu(opened[c], c)
        quantize_h(0)
        for c in range(CHUNKS // 2, CHUNKS):
            acc = bank_tile([P, PACK, CHUNK], f"h_acc{c}", c - CHUNKS // 2)
            for a in range(PASSES):
                hidden_pass(acc, c, a)
            relu(acc, c)
        quantize_h(1)

        def half_of(ap, half):
            return ap[:, half * HALF : (half + 1) * HALF]

        def piece_of(pieces, i):
            u = [first <= i < end for first, end in pieces].index(True)
            return u, (i - pieces[u][0]) * P

        def picked_tile(name, shape):
            return keep.tile(shape, U32, name=name, align_bytes=ALIGN)

        def gather_state(i, j0, end, picked):
            nc.vector.tensor_copy(picked, state[i][:].bitcast(U32).indirect(listed(j0, end - j0)))

        def rate(i, half, bank):
            u, n0 = piece_of(WA_PIECES, i)
            a_acc = bank_tile([P, HALF], "a_acc", bank)
            nc.tensor.matmul_mx(
                out=a_acc[:],
                lhsT=wa_w[u][:, 2 * n0 : 2 * (n0 + P)].bitcast(FP4X4),
                lhsT_scale=wa_s[:].bitcast(U8)[:, i * P : (i + 1) * P],
                rhs=half_of(h_q, half).bitcast(FP8X4),
                rhs_scale=half_of(h_s, half),
                start=True,
                stop=True,
            )
            nc.scalar.activation(half_of(new[i], half), a_acc[:], ACT.Exp)

        def decay(i, half):
            nc.scalar.activation(half_of(new[i], half), half_of(new[i], half), ACT.Exp, scale=-1.0)

        def times_state(decays, picked):
            nc.gpsimd.tensor_tensor(decays, picked.bitcast(F32), decays, ALU.mult)

        def token_product(i, j0, width, bank):
            b_acc = bank_tile([P, width], "b_acc", bank)
            u, n0 = piece_of(WB_PIECES, i)
            done = 0
            for columns in (HALF, QUARTER, CHUNK):
                if width & columns:
                    cols = slice(j0 + done, j0 + done + columns)
                    for a in range(PASSES):
                        nc.tensor.matmul_mx(
                            out=b_acc[:, done : done + columns],
                            lhsT=wb_w[u][:, a, n0 : n0 + P].bitcast(FP8X4),
                            lhsT_scale=wb_s[WB_FIRST:, a, :].bitcast(U8)[:, i * P : (i + 1) * P],
                            rhs=v_w[a][:, cols].bitcast(FP8X4),
                            rhs_scale=v_s[a][V_FIRST[a] :, :].bitcast(U8)[:, cols],
                            start=(a == 0),
                            stop=(a == PASSES - 1),
                        )
                    done += columns
            return b_acc

        def store(i, j0, end):
            nc.sync.dma_start(out[i * P : (i + 1) * P, j0:end], new[i][:, j0:end])

        scalar_banks = [6, 7, 5]
        vector_banks = [0, 1, 4, 2, 3]

        def turn(banks):
            banks.append(banks.pop(0))
            return banks[-1]

        def add_on_vector(i, j0, end, banks):
            dst = new[i][:, j0:end]
            nc.vector.tensor_tensor(dst, dst, token_product(i, j0, end - j0, turn(banks))[:], ALU.add)

        def add_piece(u):
            for i in range(*WB_PIECES[u]):
                for half in range(2):
                    add_on_vector(i, half * HALF, (half + 1) * HALF, vector_banks)
                store(i, 0, S)

        picked_pair = picked_tile("picked_pair", [P, 2, S])
        for i in range(2):
            for j0, end in ((0, CUT), (CUT, S)):
                gather_state(i, j0, end, picked_pair[:, i, j0:end])
            rate(i, 0, 4 + i)
        for i in range(2):
            decay(i, 0)
            times_state(half_of(new[i], 0), picked_pair[:, i, :HALF])
        for i in range(2):
            rate(i, 1, turn(scalar_banks))
        for i in range(2):
            decay(i, 1)
        times_state(new_pair[:, :, HALF:], picked_pair[:, :, HALF:])
        add_on_vector(1, GPSIMD_SHARE, S, vector_banks)
        store(1, GPSIMD_SHARE, S)

        for i in range(2, LAST):
            picked = picked_tile(f"picked{i}", [P, S])
            gather_state(i, 0, S, picked[:])
            for half in range(2):
                rate(i, half, turn(scalar_banks))
            for half in range(2):
                decay(i, half)
            times_state(new[i], picked[:])
            if i == GPSIMD_SUM_BEHIND:
                b_copy = keep.tile([P, S + GPSIMD_SHARE], F32, name="b_copy")
                for half in range(2):
                    nc.scalar.copy(half_of(b_copy, half), token_product(0, half * HALF, HALF, turn(scalar_banks))[:])
                nc.scalar.copy(b_copy[:, S:], token_product(1, 0, GPSIMD_SHARE, turn(scalar_banks))[:])
                dst = new_pair[:].rearrange("p i s -> p (i s)")[:, : S + GPSIMD_SHARE]
                nc.gpsimd.tensor_tensor(dst, b_copy[:], dst, ALU.add)
                store(0, 0, S)
                store(1, 0, GPSIMD_SHARE)
            if i > FIRST_WB_BEHIND:
                add_piece(i - FIRST_WB_BEHIND)

        between = WB_PIECES[-1][0]
        early = picked_tile("picked_early", [P, CUT])
        gather_state(LAST, 0, CUT, early[:])
        first_half = keep.tile([P, HALF], F32, name="first_half", align_bytes=ALIGN)
        b_acc = token_product(between, 0, HALF, turn(vector_banks))
        nc.vector.tensor_tensor(first_half[:], half_of(new[between], 0), b_acc[:], ALU.add)
        nc.sync.dma_start(out[between * P : (between + 1) * P, :HALF], first_half[:])
        add_on_vector(between, HALF, S, vector_banks)
        store(between, HALF, S)
        late = new[between].bitcast(U32)[:, : S - CUT]
        gather_state(LAST, CUT, S, late)
        for half in range(2):
            rate(LAST, half, turn(scalar_banks))
        for half in range(2):
            decay(LAST, half)
        times_state(new[LAST][:, :CUT], early[:])
        times_state(new[LAST][:, CUT:], late)

        for half in range(2):
            add_on_vector(LAST - 1, half * HALF, (half + 1) * HALF, vector_banks)
            store(LAST - 1, half * HALF, (half + 1) * HALF)
        add_on_vector(LAST, 0, HALF, scalar_banks)
        add_on_vector(LAST, HALF, CUT, scalar_banks)
        store(LAST, 0, CUT)
        add_on_vector(LAST, CUT, S, scalar_banks)
        store(LAST, CUT, S)
